import numpy as np
import ml_dtypes


def mxq(x, axis, fmt="e4m3"):
    dtype, down = {"e4m3": (ml_dtypes.float8_e4m3fn, 7), "e5m2": (ml_dtypes.float8_e5m2, 14)}[fmt]
    v = np.moveaxis(np.asarray(x, np.float32).astype(ml_dtypes.bfloat16).astype(np.float64), axis, -1)
    blocks = v.reshape(v.shape[:-1] + (-1, 32))
    amax = np.abs(blocks).max(-1, keepdims=True)
    byte = np.maximum(np.where(amax > 0, np.frexp(amax)[1] - 1 + 127, 0) - down, 1)
    scale = np.exp2(byte - 127.0)
    codes = (blocks / scale).astype(np.float32).astype(dtype).astype(np.float64)
    return np.moveaxis((codes * scale).reshape(v.shape), -1, axis)


WIDE = False


def mx_kscale(k):
    if not WIDE:
        return np.ones(k)
    levels = np.array([10, -10, 5, -5, 0])
    if k % 512:
        return np.exp2(np.random.permutation(np.resize(levels, k // 32))).repeat(32)
    a = np.empty((k // 512, 16))
    for p in range(k // 512):
        a[p, :8] = np.random.permutation(np.resize(levels, 8))
        for g in range(8):
            far = levels[np.abs(levels - a[p, g]) >= 10]
            a[p, g + 8] = far[np.random.randint(len(far))]
    return np.exp2(a.ravel()).repeat(32)


BF16 = ml_dtypes.bfloat16


def bf(x):
    return np.asarray(x, np.float32).astype(BF16)


def f64(x):
    return np.asarray(x).astype(np.float64)


E2M1 = np.array([0.0, 0.5, 1.0, 1.5, 2.0, 3.0, 4.0, 6.0, -0.0, -0.5, -1.0, -1.5, -2.0, -3.0, -4.0, -6.0])


def pack_weight(w, fmt):
    k, n = w.shape
    w = f64(bf(w)).reshape(k // 32, 32, n)
    amax = np.abs(w).max(1)
    if fmt == "e4m3":
        byte = np.frexp(amax)[1] - 1 + 127 - 7
    else:
        mant, ex = np.frexp(amax / 6.0)
        byte = np.where(mant > 0.5, ex, ex - 1) + 127
    byte = np.clip(np.where(amax > 0, byte, 1), 1, 254)
    scaled = (w * np.exp2(127.0 - byte)[:, None, :]).reshape(k, n).astype(np.float32)
    by_word = np.ascontiguousarray(scaled.reshape(k // 512, 128, 4, n).transpose(0, 1, 3, 2))
    if fmt == "e4m3":
        words = by_word.astype(ml_dtypes.float8_e4m3fn).view(np.uint8)
    else:
        c = by_word.astype(ml_dtypes.float4_e2m1fn).view(np.uint8) & 0xF
        words = c[..., 0::2] | (c[..., 1::2] << 4)
    return np.ascontiguousarray(words), np.ascontiguousarray(byte.astype(np.uint8).reshape(k // 512, 16, n))


def unpack_weight(words, scales, fmt):
    g, p, n, _ = words.shape
    if fmt == "e4m3":
        vals = np.ascontiguousarray(words).view(ml_dtypes.float8_e4m3fn).astype(np.float64)
    else:
        nib = np.empty((g, p, n, 4), np.uint8)
        nib[..., 0::2] = words & 0xF
        nib[..., 1::2] = words >> 4
        vals = E2M1[nib]
    vals = vals * np.repeat(np.exp2(scales.astype(np.float64) - 127.0), 8, axis=1)[..., None]
    return vals.transpose(0, 1, 3, 2).reshape(g * 512, n)
def pack4(w):
    words, scales = pack_weight(w, "e2m1")
    return words.reshape(words.shape[0], 128, -1), scales


def unpack4(words, scales):
    return unpack_weight(words.reshape(words.shape[0], 128, -1, 2), scales, "e2m1")


E4M3FN = np.array([(-1.0 if i & 128 else 1.0) * ((1.0 + (i & 7) / 8.0) * 2.0 ** (((i >> 3) & 15) - 7) if i & 120 else (i & 7) * 2.0 ** -9) for i in range(256)])


def e4m3fn_bytes(y):
    return np.clip(np.asarray(y, np.float64), -448.0, 448.0).astype(np.float32).astype(ml_dtypes.float8_e4m3fn).view(np.uint8)


def e4m3fn_values(b):
    return E4M3FN[b]


V, T, R, C, BLK = 4096, 512, 1024, 2048, 128


def setup_inputs():
    s, t = mx_kscale(V), mx_kscale(R)
    rate = 0.5 + np.random.exponential(1.0, (V, 1))
    counts = np.random.poisson(rate, (V, T))
    b = np.random.standard_normal((R, V)) / np.sqrt(V) / s
    basis_scale = (np.abs(b).reshape(R, V // BLK, BLK).max(axis=2) / 448).astype(np.float32)
    basis_bytes = e4m3fn_bytes(b / np.repeat(f64(basis_scale), BLK, axis=1))
    cat_words, cat_scales = pack4(np.random.standard_normal((R, C)) / np.sqrt(R) / t[:, None])
    return {"counts": bf(counts),
            "term_weight": bf((1 + 0.1 * np.random.standard_normal(V)) * s),
            "basis_bytes": basis_bytes,
            "basis_scale": basis_scale,
            "dir_weight": bf((1 + 0.1 * np.random.standard_normal(R)) * t),
            "cat_words": cat_words,
            "cat_scales": cat_scales}


def reference(counts, term_weight, basis_bytes, basis_scale, dir_weight, cat_words, cat_scales):
    a = np.log(f64(counts) + 1.0) * f64(term_weight)[:, None]
    basis = e4m3fn_values(basis_bytes) * np.repeat(f64(basis_scale), BLK, axis=1)
    z = mxq(basis, 1, "e4m3") @ mxq(a, 0, "e4m3")
    d = z * f64(dir_weight)[:, None]
    return mxq(d, 0, "e4m3").T @ unpack4(cat_words, cat_scales)

@@ -1,0 +1,382 @@
+from contextlib import ExitStack
+
+import concourse.mybir as mybir
+from concourse.masks import make_identity
+
+V, T, R, C = 4096, 512, 1024, 2048
+FLOPS = 2 * V * T * R + 2 * T * R * C
+
+F32 = mybir.dt.float32
+BF16 = mybir.dt.bfloat16
+U32 = mybir.dt.uint32
+I32 = mybir.dt.int32
+U8 = mybir.dt.uint8
+FP8 = mybir.dt.float8_e4m3fn
+E4M3 = mybir.dt.float8_e4m3fn_x4
+E2M1 = mybir.dt.float4_e2m1fn_x4
+MULT = mybir.AluOpType.mult
+ACT = mybir.ActivationFunctionType
+
+P = 128
+PACK = 4
+K_PASS = P * PACK
+PASSES = V // K_PASS
+BLK = 128
+BLOCKS = K_PASS // BLK
+GROUPS = R // K_PASS
+CHUNKS = 2
+TC = T // CHUNKS
+
+
+def tile_latent_term_projection_d4_kernel(
+    tc, counts, term_weight, basis_bytes, basis_scale, dir_weight, cat_words, cat_scales, out
+):
+    nc = tc.nc
+    with ExitStack() as ctx:
+        keep = ctx.enter_context(tc.tile_pool(name="keep", bufs=1))
+        flow = ctx.enter_context(tc.tile_pool(name="flow", bufs=3))
+        psum = ctx.enter_context(tc.psum_pool(name="psum", bufs=1))
+
+        ident = keep.tile([P, P], F32, name="ident")
+        scale = keep.tile([P, GROUPS, PACK, V // BLK], F32, name="scale")
+        tw = keep.tile([P, PASSES, PACK], BF16, name="tw")
+        dw16 = keep.tile([P, GROUPS, PACK], BF16, name="dw16")
+        dw = keep.tile([P, GROUPS, PACK], F32, name="dw")
+        a_codes = [keep.tile([P, PASSES, TC], U32, name="a_codes%d" % c, align_bytes=64) for c in range(CHUNKS)]
+        a_planes = [keep.tile([P, PASSES, TC], U8, name="a_planes%d" % c, align_bytes=64) for c in range(CHUNKS)]
+        b_codes = keep.tile([P, 32, 256], U32, name="b_codes", align_bytes=64)
+        b_planes = keep.tile([P, 32, 256], U8, name="b_planes", align_bytes=64)
+        d_codes = [keep.tile([P, GROUPS, TC], U32, name="d_codes%d" % c, align_bytes=64) for c in range(CHUNKS)]
+        d_planes = [keep.tile([P, GROUPS, TC], U8, name="d_planes%d" % c, align_bytes=64) for c in range(CHUNKS)]
+        cat = keep.tile([P, GROUPS, 2 * C], U8, name="cat", align_bytes=64)
+        cat_planes = keep.tile([P, GROUPS, C], U8, name="cat_planes", align_bytes=64)
+
+        bytes_view = basis_bytes.rearrange("(g m j) k -> g m j k", g=GROUPS, j=PACK)
+        counts_view = counts.rearrange("(g p j) w -> g p j w", p=P, j=PACK)
+
+        byt = {}
+
+        def load_bytes(gr, j0, j1, k0, k1):
+            held = keep.tile([P, j1 - j0, k1 - k0], U8, name="byt_%d_%d_%d" % (gr, j0, k0))
+            nc.sync.dma_start(out=held[:], in_=bytes_view[gr, :, j0:j1, k0:k1])
+            for j in range(j0, j1):
+                for b in range(k0 // BLK, k1 // BLK):
+                    byt[(gr, j, b)] = held[:, j - j0, b * BLK - k0 : (b + 1) * BLK - k0]
+
+        raw = {}
+
+        def load_counts(g):
+            raw[g] = flow.tile([P, PACK, T], BF16, name="raw", tag="raw", bufs=8)
+            nc.sync.dma_start(out=raw[g][:], in_=counts_view[g])
+
+        logs, a_bf = {}, {}
+
+        def ln_part(c, g, j0, j1):
+            if j0 == 0:
+                logs[(c, g)] = flow.tile([P, PACK, TC], F32, name="logs", tag="logs", bufs=3)
+            nc.scalar.activation(
+                out=logs[(c, g)][:, j0:j1, :],
+                in_=raw[g][:, j0:j1, c * TC : (c + 1) * TC],
+                func=ACT.Ln,
+                bias=1.0,
+                scale=1.0,
+            )
+
+        def weigh_part(c, g, h, parts):
+            if h == 0:
+                a_bf[(c, g)] = flow.tile([P, TC, PACK], BF16, name="a_bf", tag="a_bf", bufs=3, align_bytes=64)
+            n = TC // parts
+            docs = slice(h * n, (h + 1) * n)
+            nc.vector.tensor_tensor(
+                out=a_bf[(c, g)][:, docs, :].rearrange("p (c i) j -> p c j i", i=4),
+                in0=logs[(c, g)][:, :, docs].rearrange("p j (c i) -> p c j i", i=4),
+                in1=tw[:, g, :].unsqueeze(1).unsqueeze(3).to_broadcast([P, n // 4, PACK, 4]),
+                op=MULT,
+            )
+
+        def quantize_a(c, g):
+            nc.vector.quantize_mx(
+                out=a_codes[c][:, g, :].bitcast(E4M3),
+                scales=a_planes[c][:, g, :],
+                in_=a_bf[(c, g)][:].rearrange("p w j -> p (w j)"),
+            )
+
+        units = [((2 * i, g), (2 * i + 1, g)) for g in range(PASSES) for i in range(3)]
+        units += [((rt, 2 * i), (rt, 2 * i + 1)) for rt in (6, 7) for i in range(4)]
+        home = {}
+        for n, unit in enumerate(units):
+            for h, tile_of in enumerate(unit):
+                home[tile_of] = (n, h)
+        wide, turned, grouped = {}, {}, {}
+
+        def widen(n, on_scalar):
+            wide[n] = flow.tile([P, 2, K_PASS], BF16, name="wide", tag="wide", bufs=4)
+            i = 0
+            for h, (rt, g) in enumerate(units[n]):
+                gr, j = divmod(rt, PACK)
+                for q in range(BLOCKS):
+                    b = BLOCKS * g + q
+                    dst = wide[n][:, h, q * BLK : (q + 1) * BLK]
+                    src = byt[(gr, j, b)].bitcast(FP8)
+                    factor = scale[:, gr, j, b : b + 1]
+                    if i >= 2 * BLOCKS - on_scalar:
+                        nc.scalar.activation(out=dst, in_=src, func=ACT.Copy, scale=factor)
+                    else:
+                        nc.vector.tensor_scalar(out=dst, in0=src, scalar1=factor, scalar2=None, op0=MULT)
+                    i += 1
+
+        def turn(n, bank):
+            turned[n] = psum.tile([P, 2, 2, P], F32, name="turned", tag="b%d" % bank)
+            for h in range(2):
+                words = wide[n][:, h, :].bitcast(F32)
+                for u in range(2):
+                    nc.tensor.transpose(turned[n][:, h, u, :], words[:, u : K_PASS // 2 : 2], ident[:])
+
+        def collect(n, on_vector):
+            grouped[n] = flow.tile([P, 2, P, PACK], BF16, name="grouped", tag="grouped", bufs=4, align_bytes=64)
+            dst = grouped[n][:].rearrange("p h r j -> p (h r j)").bitcast(F32).rearrange("p (h r u) -> p h r u", h=2, u=2)
+            src = turned[n][:].rearrange("p h u r -> p h r u")
+            if on_vector:
+                nc.vector.tensor_copy(out=dst, in_=src)
+            else:
+                nc.scalar.copy(out=dst, in_=src)
+
+        def quantize_b(n):
+            nc.vector.quantize_mx(
+                out=b_codes[:, n, :].bitcast(E4M3),
+                scales=b_planes[:, n, :],
+                in_=grouped[n][:].rearrange("p h r j -> p (h r j)"),
+            )
+
+        z = {}
+
+        def multiply(c, rt, g, bank):
+            at, h = home[(rt, g)]
+            cols = slice(h * P, (h + 1) * P)
+            if g == 0:
+                z[(c, rt)] = psum.tile([P, TC], F32, name="z", tag="b%d" % bank)
+            nc.tensor.matmul_mx(
+                out=z[(c, rt)][:],
+                lhsT=b_codes[:, at, cols].bitcast(E4M3),
+                lhsT_scale=b_planes[:, at, cols],
+                rhs=a_codes[c][:, g, :].bitcast(E4M3),
+                rhs_scale=a_planes[c][:, g, :],
+                start=(g == 0),
+                stop=(g == PASSES - 1),
+            )
+
+        def multiply_unit(n):
+            for rt, g in units[n]:
+                multiply(0, rt, g, rt if rt < 6 else rt - 6)
+
+        dz, d_bf = {}, {}
+
+        def weigh_z(c, rt, on_vector):
+            gr, j = divmod(rt, PACK)
+            if j == 0:
+                dz[(c, gr)] = flow.tile([P, PACK, TC], BF16, name="dz", tag="dz", bufs=2)
+                d_bf[(c, gr)] = flow.tile([P, TC, PACK], BF16, name="d_bf", tag="d_bf", bufs=2, align_bytes=64)
+            dst = dz[(c, gr)][:, j, :]
+            if on_vector:
+                nc.vector.tensor_scalar(out=dst, in0=z[(c, rt)][:], scalar1=dw[:, gr, j : j + 1], scalar2=None, op0=MULT)
+            else:
+                nc.scalar.activation(out=dst, in_=z[(c, rt)][:], func=ACT.Copy, scale=dw[:, gr, j : j + 1])
+
+        def interleave_d(c, gr, h, parts):
+            n = TC // parts
+            docs = slice(h * n, (h + 1) * n)
+            nc.vector.tensor_copy(
+                out=d_bf[(c, gr)][:, docs, :].rearrange("p (c i) j -> p c j i", i=4),
+                in_=dz[(c, gr)][:, :, docs].rearrange("p j (c i) -> p c j i", i=4),
+            )
+
+        def quantize_d(c, gr, h, parts):
+            n = TC // parts
+            docs = slice(h * n, (h + 1) * n)
+            nc.vector.quantize_mx(
+                out=d_codes[c][:, gr, docs].bitcast(E4M3),
+                scales=d_planes[c][:, gr, docs],
+                in_=d_bf[(c, gr)][:, docs, :].rearrange("p w j -> p (w j)"),
+            )
+
+        o, o_sb = {}, {}
+
+        def score(c, i, gr, bank=None):
+            dt, cc = divmod(i, 4)
+            if gr == 0:
+                o[(c, i)] = psum.tile([P, 512], F32, name="o", tag="b%d" % bank)
+            docs = slice(dt * P, (dt + 1) * P)
+            nc.tensor.matmul_mx(
+                out=o[(c, i)][:],
+                lhsT=d_codes[c][:, gr, docs].bitcast(E4M3),
+                lhsT_scale=d_planes[c][:, gr, docs],
+                rhs=cat[:, gr, cc * 1024 : (cc + 1) * 1024].bitcast(E2M1),
+                rhs_scale=cat_planes[:, gr, cc * 512 : (cc + 1) * 512],
+                start=(gr == 0),
+                stop=(gr == 1),
+            )
+
+        def emit(c, i, on_vector):
+            dt, cc = divmod(i, 4)
+            if cc % 2 == 0:
+                o_sb[(c, i // 2)] = flow.tile([P, 1024], F32, name="o_sb", tag="o_sb", bufs=8)
+            dst = o_sb[(c, i // 2)][:, (cc % 2) * 512 : (cc % 2 + 1) * 512]
+            if on_vector:
+                nc.vector.tensor_copy(out=dst, in_=o[(c, i)][:])
+            else:
+                nc.scalar.copy(out=dst, in_=o[(c, i)][:])
+            if cc % 2:
+                row = c * TC + dt * P
+                nc.sync.dma_start(out=out[row : row + P, (cc - 1) * 512 : (cc + 1) * 512], in_=o_sb[(c, i // 2)][:])
+
+        with tc.manual_schedule():
+            nc.sync.dma_start(out=scale[:], in_=basis_scale.rearrange("(g m j) b -> m g j b", g=GROUPS, j=PACK))
+            load_bytes(0, 0, 4, 0, 512)
+            load_counts(0)
+            nc.scalar.dma_start(out=tw[:], in_=term_weight.rearrange("(g p j) -> p g j", p=P, j=PACK))
+            load_bytes(1, 0, 2, 0, 512)
+            load_counts(1)
+            load_bytes(0, 0, 4, 512, 1024)
+            load_bytes(1, 0, 2, 512, 1024)
+            nc.scalar.dma_start(out=dw16[:], in_=dir_weight.rearrange("(g m j) -> m g j", g=GROUPS, j=PACK))
+            load_counts(2)
+            for k0 in range(1024, V, 1024):
+                load_bytes(0, 0, 4, k0, k0 + 1024)
+                load_bytes(1, 0, 2, k0, k0 + 1024)
+                load_counts(k0 // 512 + 1)
+                if k0 // 512 + 2 < PASSES:
+                    load_counts(k0 // 512 + 2)
+            for k0 in range(0, V, 2048):
+                load_bytes(1, 2, 4, k0, k0 + 2048)
+            nc.sync.dma_start(
+                out=cat[:].rearrange("p g n -> p (g n)").bitcast(I32).rearrange("p (g n) -> p g n", g=GROUPS),
+                in_=cat_words.bitcast(I32).rearrange("g p n -> p g n"),
+            )
+            planes_i32 = cat_planes[:].rearrange("p g n -> p (g n)").bitcast(I32)
+            nc.vector.memset(planes_i32, 0)
+            for quad in range(4):
+                nc.sync.dma_start(
+                    out=planes_i32[32 * quad : 32 * quad + 4, :].rearrange("p (g n) -> p g n", g=GROUPS),
+                    in_=cat_scales[:, 4 * quad : 4 * quad + 4, :].bitcast(I32).rearrange("g q n -> q g n"),
+                )
+            make_identity(nc, ident[:])
+
+            ln_part(0, 0, 0, 2)
+            ln_part(0, 0, 2, 4)
+            widen(0, 2)
+            for s in range(24):
+                g, i = divmod(s, 3)
+                widen(s + 1, 3 if i == 2 else 2)
+                if i < 2:
+                    weigh_part(0, g, i, 2)
+                if i > 0 and g + 1 < PASSES:
+                    ln_part(0, g + 1, 2 * i - 2, 2 * i)
+                if s >= 1:
+                    collect(s - 1, False)
+                if i == 2:
+                    quantize_a(0, g)
+                if s >= 2:
+                    quantize_b(s - 2)
+                turn(s, 6 + s % 2)
+                if s >= 3:
+                    multiply_unit(s - 3)
+            nc.vector.tensor_copy(out=dw[:], in_=dw16[:])
+            widen(25, 3)
+            turn(24, 6)
+            collect(23, False)
+            turn(25, 7)
+            quantize_b(22)
+            multiply_unit(21)
+            multiply_unit(22)
+            quantize_b(23)
+            for p in range(4):
+                n = 24 + 2 * p
+                if p < 3:
+                    widen(n + 2, 3)
+                    widen(n + 3, 3)
+                if p == 0:
+                    multiply_unit(23)
+                    for rt in range(4):
+                        weigh_z(0, rt, rt % 2 == 1)
+                collect(n, False)
+                collect(n + 1, True)
+                if p == 0:
+                    for rt in range(4, 6):
+                        weigh_z(0, rt, rt % 2 == 1)
+                if p < 3:
+                    for m in range(n + 2, n + 4):
+                        turn(m, (6 if p % 2 == 1 else 2) + m % 2)
+                if p == 3:
+                    weigh_z(0, 6, False)
+                ln_part(1, p, 0, 4)
+                quantize_b(n)
+                if p == 0:
+                    interleave_d(0, 0, 0, 1)
+                quantize_b(n + 1)
+                if p == 1:
+                    quantize_d(0, 0, 0, 1)
+                weigh_part(1, p, 0, 1)
+                multiply_unit(n)
+                multiply_unit(n + 1)
+                if p > 0:
+                    quantize_a(1, p - 1)
+            bank_b = [2, 3, 0, 1, 4, 5, 6, 7]
+
+            def multiply_b(rts, passes):
+                for g in passes:
+                    for rt in rts:
+                        multiply(1, rt, g, bank_b[rt])
+
+            for i in range(4):
+                score(0, i, 0, 4 + i)
+            multiply_b((0, 1), range(3))
+            weigh_z(0, 7, False)
+            interleave_d(0, 1, 0, 1)
+            quantize_a(1, 3)
+            quantize_d(0, 1, 0, 1)
+            ln_part(1, 4, 0, 4)
+            ln_part(1, 5, 0, 4)
+            weigh_part(1, 4, 0, 1)
+            for i in range(4):
+                score(0, i, 1)
+            multiply_b((2, 3), range(3))
+            for i in range(4):
+                emit(0, i, i % 2 == 1)
+            weigh_part(1, 5, 0, 1)
+            quantize_a(1, 4)
+            for i in range(4, 8):
+                score(0, i, 0, i)
+                score(0, i, 1)
+            multiply_b(range(4), range(3, 5))
+            ln_part(1, 6, 0, 4)
+            quantize_a(1, 5)
+            for i in range(4, 8):
+                emit(0, i, i % 2 == 1)
+            weigh_part(1, 6, 0, 1)
+            ln_part(1, 7, 0, 4)
+            weigh_part(1, 7, 0, 1)
+            quantize_a(1, 6)
+            quantize_a(1, 7)
+            multiply_b(range(4), range(5, 6))
+            multiply_b(range(4, 8), range(6))
+            multiply_b(range(4), range(6, 8))
+            multiply_b(range(4, 8), range(6, 8))
+            for rt in range(8):
+                weigh_z(1, rt, rt % 2 == 1)
+                if rt == 5:
+                    for h in range(2):
+                        interleave_d(1, 0, h, 2)
+                if rt == 7:
+                    for h in range(2):
+                        quantize_d(1, 0, h, 2)
+            for h in range(2):
+                interleave_d(1, 1, h, 2)
+            for h in range(2):
+                quantize_d(1, 1, h, 2)
+            for i in range(4):
+                score(1, i, 0, bank_b[i])
+            for i in range(8):
+                score(1, i, 1)
+                if i + 4 < 8:
+                    score(1, i + 4, 0, bank_b[i + 4])
+                emit(1, i, i % 2 == 1)

@@ -24,8 +24,7 @@ PASSES = V // K_PASS
 BLK = 128
 BLOCKS = K_PASS // BLK
 GROUPS = R // K_PASS
-CHUNKS = 2
-TC = T // CHUNKS
+HALF = T // 2
 
 
 def tile_latent_term_projection_d4_kernel(
@@ -42,12 +41,12 @@ def tile_latent_term_projection_d4_kernel(
         tw = keep.tile([P, PASSES, PACK], BF16, name="tw")
         dw16 = keep.tile([P, GROUPS, PACK], BF16, name="dw16")
         dw = keep.tile([P, GROUPS, PACK], F32, name="dw")
-        a_codes = [keep.tile([P, PASSES, TC], U32, name="a_codes%d" % c, align_bytes=64) for c in range(CHUNKS)]
-        a_planes = [keep.tile([P, PASSES, TC], U8, name="a_planes%d" % c, align_bytes=64) for c in range(CHUNKS)]
+        a_codes = keep.tile([P, PASSES, T], U32, name="a_codes", align_bytes=64)
+        a_planes = keep.tile([P, PASSES, T], U8, name="a_planes", align_bytes=64)
         b_codes = keep.tile([P, 32, 256], U32, name="b_codes", align_bytes=64)
         b_planes = keep.tile([P, 32, 256], U8, name="b_planes", align_bytes=64)
-        d_codes = [keep.tile([P, GROUPS, TC], U32, name="d_codes%d" % c, align_bytes=64) for c in range(CHUNKS)]
-        d_planes = [keep.tile([P, GROUPS, TC], U8, name="d_planes%d" % c, align_bytes=64) for c in range(CHUNKS)]
+        d_codes = keep.tile([P, GROUPS, T], U32, name="d_codes", align_bytes=64)
+        d_planes = keep.tile([P, GROUPS, T], U8, name="d_planes", align_bytes=64)
         cat = keep.tile([P, GROUPS, 2 * C], U8, name="cat", align_bytes=64)
         cat_planes = keep.tile([P, GROUPS, C], U8, name="cat_planes", align_bytes=64)
 
@@ -69,36 +68,40 @@ def tile_latent_term_projection_d4_kernel(
             raw[g] = flow.tile([P, PACK, T], BF16, name="raw", tag="raw", bufs=8)
             nc.sync.dma_start(out=raw[g][:], in_=counts_view[g])
 
+        free_banks = ["b%d" % i for i in range(8)]
+        held = {}
+
+        def take(shape, key):
+            held[key] = free_banks.pop(0)
+            return psum.tile(shape, F32, name="bank", tag=held[key])
+
+        def give(key):
+            free_banks.append(held[key])
+
         logs, a_bf = {}, {}
 
-        def ln_part(c, g, j0, j1):
-            if j0 == 0:
-                logs[(c, g)] = flow.tile([P, PACK, TC], F32, name="logs", tag="logs", bufs=3)
-            nc.scalar.activation(
-                out=logs[(c, g)][:, j0:j1, :],
-                in_=raw[g][:, j0:j1, c * TC : (c + 1) * TC],
-                func=ACT.Ln,
-                bias=1.0,
-                scale=1.0,
-            )
+        def ln_part(g, k):
+            if k == 0:
+                logs[g] = flow.tile([P, PACK, T], F32, name="logs", tag="logs", bufs=3)
+            js = slice(2 * k, 2 * k + 2)
+            nc.scalar.activation(out=logs[g][:, js, :], in_=raw[g][:, js, :], func=ACT.Ln, bias=1.0, scale=1.0)
 
-        def weigh_part(c, g, h, parts):
-            if h == 0:
-                a_bf[(c, g)] = flow.tile([P, TC, PACK], BF16, name="a_bf", tag="a_bf", bufs=3, align_bytes=64)
-            n = TC // parts
-            docs = slice(h * n, (h + 1) * n)
+        def weigh_part(g, k):
+            if k == 0:
+                a_bf[g] = flow.tile([P, T, PACK], BF16, name="a_bf", tag="a_bf", bufs=3, align_bytes=64)
+            docs = slice(k * HALF, (k + 1) * HALF)
             nc.vector.tensor_tensor(
-                out=a_bf[(c, g)][:, docs, :].rearrange("p (c i) j -> p c j i", i=4),
-                in0=logs[(c, g)][:, :, docs].rearrange("p j (c i) -> p c j i", i=4),
-                in1=tw[:, g, :].unsqueeze(1).unsqueeze(3).to_broadcast([P, n // 4, PACK, 4]),
+                out=a_bf[g][:, docs, :].rearrange("p (c i) j -> p c j i", i=4),
+                in0=logs[g][:, :, docs].rearrange("p j (c i) -> p c j i", i=4),
+                in1=tw[:, g, :].unsqueeze(1).unsqueeze(3).to_broadcast([P, HALF // 4, PACK, 4]),
                 op=MULT,
             )
 
-        def quantize_a(c, g):
+        def quantize_a(g):
             nc.vector.quantize_mx(
-                out=a_codes[c][:, g, :].bitcast(E4M3),
-                scales=a_planes[c][:, g, :],
-                in_=a_bf[(c, g)][:].rearrange("p w j -> p (w j)"),
+                out=a_codes[:, g, :].bitcast(E4M3),
+                scales=a_planes[:, g, :],
+                in_=a_bf[g][:].rearrange("p w j -> p (w j)"),
             )
 
         units = [((2 * i, g), (2 * i + 1, g)) for g in range(PASSES) for i in range(3)]
@@ -107,39 +110,47 @@ def tile_latent_term_projection_d4_kernel(
         for n, unit in enumerate(units):
             for h, tile_of in enumerate(unit):
                 home[tile_of] = (n, h)
-        wide, turned, grouped = {}, {}, {}
+        wide, turned, grouped, by_scalar = {}, {}, {}, {}
 
-        def widen(n, on_scalar):
-            wide[n] = flow.tile([P, 2, K_PASS], BF16, name="wide", tag="wide", bufs=4)
-            i = 0
-            for h, (rt, g) in enumerate(units[n]):
-                gr, j = divmod(rt, PACK)
-                for q in range(BLOCKS):
-                    b = BLOCKS * g + q
-                    dst = wide[n][:, h, q * BLK : (q + 1) * BLK]
-                    src = byt[(gr, j, b)].bitcast(FP8)
-                    factor = scale[:, gr, j, b : b + 1]
-                    if i >= 2 * BLOCKS - on_scalar:
-                        nc.scalar.activation(out=dst, in_=src, func=ACT.Copy, scale=factor)
-                    else:
-                        nc.vector.tensor_scalar(out=dst, in0=src, scalar1=factor, scalar2=None, op0=MULT)
-                    i += 1
+        def widen(n, h, on_scalar):
+            if h == 0:
+                wide[n] = flow.tile([P, 2, K_PASS], BF16, name="wide", tag="wide", bufs=4)
+            by_scalar[(n, h)] = on_scalar
+            rt, g = units[n][h]
+            gr, j = divmod(rt, PACK)
+            by_word = wide[n][:, h, :].rearrange("p (u w e) -> p w u e", u=2, e=2)
+            for q in range(BLOCKS):
+                b = BLOCKS * g + q
+                src = byt[(gr, j, b)].bitcast(FP8)
+                factor = scale[:, gr, j, b : b + 1]
+                if on_scalar:
+                    nc.scalar.activation(out=wide[n][:, h, q * BLK : (q + 1) * BLK], in_=src, func=ACT.Copy, scale=factor)
+                else:
+                    nc.vector.tensor_scalar(
+                        out=by_word[:, 32 * q : 32 * q + 32, :, :],
+                        in0=src.rearrange("p (w u e) -> p w u e", u=2, e=2),
+                        scalar1=factor,
+                        scalar2=None,
+                        op0=MULT,
+                    )
 
-        def turn(n, bank):
-            turned[n] = psum.tile([P, 2, 2, P], F32, name="turned", tag="b%d" % bank)
+        def turn(n):
+            turned[n] = take([P, 2, 2, P], ("turned", n))
             for h in range(2):
                 words = wide[n][:, h, :].bitcast(F32)
                 for u in range(2):
-                    nc.tensor.transpose(turned[n][:, h, u, :], words[:, u : K_PASS // 2 : 2], ident[:])
+                    picked = words[:, u : 2 * P : 2] if by_scalar[(n, h)] else words[:, u * P : (u + 1) * P]
+                    nc.tensor.transpose(turned[n][:, h, u, :], picked, ident[:])
 
         def collect(n, on_vector):
-            grouped[n] = flow.tile([P, 2, P, PACK], BF16, name="grouped", tag="grouped", bufs=4, align_bytes=64)
+            grouped[n] = flow.tile([P, 2, P, PACK], BF16, name="grouped", tag="grouped", bufs=6, align_bytes=64)
             dst = grouped[n][:].rearrange("p h r j -> p (h r j)").bitcast(F32).rearrange("p (h r u) -> p h r u", h=2, u=2)
             src = turned[n][:].rearrange("p h u r -> p h r u")
             if on_vector:
                 nc.vector.tensor_copy(out=dst, in_=src)
             else:
                 nc.scalar.copy(out=dst, in_=src)
+            give(("turned", n))
 
         def quantize_b(n):
             nc.vector.quantize_mx(
@@ -150,84 +161,83 @@ def tile_latent_term_projection_d4_kernel(
 
         z = {}
 
-        def multiply(c, rt, g, bank):
+        def multiply(rt, g, key, docs):
             at, h = home[(rt, g)]
             cols = slice(h * P, (h + 1) * P)
             if g == 0:
-                z[(c, rt)] = psum.tile([P, TC], F32, name="z", tag="b%d" % bank)
+                z[key] = take([P, docs.stop - docs.start], key)
             nc.tensor.matmul_mx(
-                out=z[(c, rt)][:],
+                out=z[key][:],
                 lhsT=b_codes[:, at, cols].bitcast(E4M3),
                 lhsT_scale=b_planes[:, at, cols],
-                rhs=a_codes[c][:, g, :].bitcast(E4M3),
-                rhs_scale=a_planes[c][:, g, :],
+                rhs=a_codes[:, g, docs].bitcast(E4M3),
+                rhs_scale=a_planes[:, g, docs],
                 start=(g == 0),
                 stop=(g == PASSES - 1),
             )
 
         def multiply_unit(n):
             for rt, g in units[n]:
-                multiply(0, rt, g, rt if rt < 6 else rt - 6)
+                if rt < 6:
+                    multiply(rt, g, ("z", rt), slice(0, T))
+                else:
+                    multiply(rt, g, ("z", rt, 0), slice(0, HALF))
 
-        dz, d_bf = {}, {}
+        def multiply_late(rt, passes):
+            for g in passes:
+                multiply(rt, g, ("z", rt, 1), slice(HALF, T))
 
-        def weigh_z(c, rt, on_vector):
+        dz = [keep.tile([P, PACK, T], BF16, name="dz%d" % gr) for gr in range(GROUPS)]
+        d_bf = [keep.tile([P, T, PACK], BF16, name="d_bf%d" % gr, align_bytes=64) for gr in range(GROUPS)]
+
+        def weigh_z(rt, key, docs, on_vector):
             gr, j = divmod(rt, PACK)
-            if j == 0:
-                dz[(c, gr)] = flow.tile([P, PACK, TC], BF16, name="dz", tag="dz", bufs=2)
-                d_bf[(c, gr)] = flow.tile([P, TC, PACK], BF16, name="d_bf", tag="d_bf", bufs=2, align_bytes=64)
-            dst = dz[(c, gr)][:, j, :]
+            dst = dz[gr][:, j, docs]
             if on_vector:
-                nc.vector.tensor_scalar(out=dst, in0=z[(c, rt)][:], scalar1=dw[:, gr, j : j + 1], scalar2=None, op0=MULT)
+                nc.vector.tensor_scalar(out=dst, in0=z[key][:], scalar1=dw[:, gr, j : j + 1], scalar2=None, op0=MULT)
             else:
-                nc.scalar.activation(out=dst, in_=z[(c, rt)][:], func=ACT.Copy, scale=dw[:, gr, j : j + 1])
+                nc.scalar.activation(out=dst, in_=z[key][:], func=ACT.Copy, scale=dw[:, gr, j : j + 1])
+            give(key)
 
-        def interleave_d(c, gr, h, parts):
-            n = TC // parts
-            docs = slice(h * n, (h + 1) * n)
+        def interleave_d(gr, docs):
             nc.vector.tensor_copy(
-                out=d_bf[(c, gr)][:, docs, :].rearrange("p (c i) j -> p c j i", i=4),
-                in_=dz[(c, gr)][:, :, docs].rearrange("p j (c i) -> p c j i", i=4),
+                out=d_bf[gr][:, docs, :].rearrange("p (c i) j -> p c j i", i=4),
+                in_=dz[gr][:, :, docs].rearrange("p j (c i) -> p c j i", i=4),
             )
 
-        def quantize_d(c, gr, h, parts):
-            n = TC // parts
-            docs = slice(h * n, (h + 1) * n)
+        def quantize_d(gr, docs):
             nc.vector.quantize_mx(
-                out=d_codes[c][:, gr, docs].bitcast(E4M3),
-                scales=d_planes[c][:, gr, docs],
-                in_=d_bf[(c, gr)][:, docs, :].rearrange("p w j -> p (w j)"),
+                out=d_codes[:, gr, docs].bitcast(E4M3),
+                scales=d_planes[:, gr, docs],
+                in_=d_bf[gr][:, docs, :].rearrange("p w j -> p (w j)"),
             )
 
-        o, o_sb = {}, {}
+        o = {}
 
-        def score(c, i, gr, bank=None):
+        def score(i, gr):
             dt, cc = divmod(i, 4)
             if gr == 0:
-                o[(c, i)] = psum.tile([P, 512], F32, name="o", tag="b%d" % bank)
+                o[i] = take([P, 512], ("o", i))
             docs = slice(dt * P, (dt + 1) * P)
             nc.tensor.matmul_mx(
-                out=o[(c, i)][:],
-                lhsT=d_codes[c][:, gr, docs].bitcast(E4M3),
-                lhsT_scale=d_planes[c][:, gr, docs],
+                out=o[i][:],
+                lhsT=d_codes[:, gr, docs].bitcast(E4M3),
+                lhsT_scale=d_planes[:, gr, docs],
                 rhs=cat[:, gr, cc * 1024 : (cc + 1) * 1024].bitcast(E2M1),
                 rhs_scale=cat_planes[:, gr, cc * 512 : (cc + 1) * 512],
                 start=(gr == 0),
                 stop=(gr == 1),
             )
 
-        def emit(c, i, on_vector):
+        def emit(i, on_vector):
             dt, cc = divmod(i, 4)
-            if cc % 2 == 0:
-                o_sb[(c, i // 2)] = flow.tile([P, 1024], F32, name="o_sb", tag="o_sb", bufs=8)
-            dst = o_sb[(c, i // 2)][:, (cc % 2) * 512 : (cc % 2 + 1) * 512]
+            o_sb = flow.tile([P, 512], F32, name="o_sb", tag="raw", bufs=8)
             if on_vector:
-                nc.vector.tensor_copy(out=dst, in_=o[(c, i)][:])
+                nc.vector.tensor_copy(out=o_sb[:], in_=o[i][:])
             else:
-                nc.scalar.copy(out=dst, in_=o[(c, i)][:])
-            if cc % 2:
-                row = c * TC + dt * P
-                nc.sync.dma_start(out=out[row : row + P, (cc - 1) * 512 : (cc + 1) * 512], in_=o_sb[(c, i // 2)][:])
+                nc.scalar.copy(out=o_sb[:], in_=o[i][:])
+            give(("o", i))
+            nc.sync.dma_start(out=out[dt * P : (dt + 1) * P, cc * 512 : (cc + 1) * 512], in_=o_sb[:])
 
         with tc.manual_schedule():
             nc.sync.dma_start(out=scale[:], in_=basis_scale.rearrange("(g m j) b -> m g j b", g=GROUPS, j=PACK))
@@ -261,122 +271,57 @@ def tile_latent_term_projection_d4_kernel(
                 )
             make_identity(nc, ident[:])
 
-            ln_part(0, 0, 0, 2)
-            ln_part(0, 0, 2, 4)
-            widen(0, 2)
-            for s in range(24):
-                g, i = divmod(s, 3)
-                widen(s + 1, 3 if i == 2 else 2)
-                if i < 2:
-                    weigh_part(0, g, i, 2)
-                if i > 0 and g + 1 < PASSES:
-                    ln_part(0, g + 1, 2 * i - 2, 2 * i)
-                if s >= 1:
-                    collect(s - 1, False)
-                if i == 2:
-                    quantize_a(0, g)
-                if s >= 2:
-                    quantize_b(s - 2)
-                turn(s, 6 + s % 2)
-                if s >= 3:
-                    multiply_unit(s - 3)
-            nc.vector.tensor_copy(out=dw[:], in_=dw16[:])
-            widen(25, 3)
-            turn(24, 6)
-            collect(23, False)
-            turn(25, 7)
-            quantize_b(22)
-            multiply_unit(21)
-            multiply_unit(22)
-            quantize_b(23)
-            for p in range(4):
-                n = 24 + 2 * p
-                if p < 3:
-                    widen(n + 2, 3)
-                    widen(n + 3, 3)
-                if p == 0:
-                    multiply_unit(23)
-                    for rt in range(4):
-                        weigh_z(0, rt, rt % 2 == 1)
-                collect(n, False)
-                collect(n + 1, True)
-                if p == 0:
-                    for rt in range(4, 6):
-                        weigh_z(0, rt, rt % 2 == 1)
-                if p < 3:
-                    for m in range(n + 2, n + 4):
-                        turn(m, (6 if p % 2 == 1 else 2) + m % 2)
-                if p == 3:
-                    weigh_z(0, 6, False)
-                ln_part(1, p, 0, 4)
-                quantize_b(n)
-                if p == 0:
-                    interleave_d(0, 0, 0, 1)
-                quantize_b(n + 1)
-                if p == 1:
-                    quantize_d(0, 0, 0, 1)
-                weigh_part(1, p, 0, 1)
-                multiply_unit(n)
-                multiply_unit(n + 1)
-                if p > 0:
-                    quantize_a(1, p - 1)
-            bank_b = [2, 3, 0, 1, 4, 5, 6, 7]
+            work = []
 
-            def multiply_b(rts, passes):
-                for g in passes:
-                    for rt in rts:
-                        multiply(1, rt, g, bank_b[rt])
+            def at(due, call, *args):
+                work.append((due, len(work), call, args))
 
-            for i in range(4):
-                score(0, i, 0, 4 + i)
-            multiply_b((0, 1), range(3))
-            weigh_z(0, 7, False)
-            interleave_d(0, 1, 0, 1)
-            quantize_a(1, 3)
-            quantize_d(0, 1, 0, 1)
-            ln_part(1, 4, 0, 4)
-            ln_part(1, 5, 0, 4)
-            weigh_part(1, 4, 0, 1)
-            for i in range(4):
-                score(0, i, 1)
-            multiply_b((2, 3), range(3))
-            for i in range(4):
-                emit(0, i, i % 2 == 1)
-            weigh_part(1, 5, 0, 1)
-            quantize_a(1, 4)
-            for i in range(4, 8):
-                score(0, i, 0, i)
-                score(0, i, 1)
-            multiply_b(range(4), range(3, 5))
-            ln_part(1, 6, 0, 4)
-            quantize_a(1, 5)
-            for i in range(4, 8):
-                emit(0, i, i % 2 == 1)
-            weigh_part(1, 6, 0, 1)
-            ln_part(1, 7, 0, 4)
-            weigh_part(1, 7, 0, 1)
-            quantize_a(1, 6)
-            quantize_a(1, 7)
-            multiply_b(range(4), range(5, 6))
-            multiply_b(range(4, 8), range(6))
-            multiply_b(range(4), range(6, 8))
-            multiply_b(range(4, 8), range(6, 8))
-            for rt in range(8):
-                weigh_z(1, rt, rt % 2 == 1)
-                if rt == 5:
-                    for h in range(2):
-                        interleave_d(1, 0, h, 2)
-                if rt == 7:
-                    for h in range(2):
-                        quantize_d(1, 0, h, 2)
+            def step(n):
+                return float(n) if n < 24 else 24 + (n - 24) * 0.821
+
+            by_s, by_v = 0.5, 0.3
+            for n in range(len(units)):
+                by_s += 0.603 if n < 24 else 0.852
+                by_v += 0 if n < 24 else 0.174
+                s_half = by_s >= 1 and n > 0
+                v_copy = by_v >= 1
+                by_s -= s_half
+                by_v -= v_copy
+                for h in range(2):
+                    at(step(n) - 0.671 + 0.02 * h, widen, n, h, s_half and h == 1)
+                at(step(n), turn, n)
+                at(step(n) + 1.359, collect, n, v_copy)
+                at(step(n) + 1.359 + 2.921, quantize_b, n)
+                at(step(n) + 1.359 + 2.921 + 1.512, multiply_unit, n)
+            at(20.0, nc.vector.tensor_copy, dw[:], dw16[:])
+            for g in range(PASSES):
+                for k in range(2):
+                    at(3 * g - 1.081 + 0.281 * k, ln_part, g, k)
+                    at(3 * g - 1.081 + 2.706 + 1.364 * k, weigh_part, g, k)
+                at(3 * g - 1.081 + 2.706 + 1.364 + 1.171, quantize_a, g)
+            last = step(31) + 1.359 + 2.921 + 1.512
+            halves = (slice(0, HALF), slice(HALF, T))
+            for rt, late in ((6, 0.601), (7, 0.855)):
+                at(last + late, multiply_late, rt, range(4))
+                at(last + late + 0.141, multiply_late, rt, range(4, 8))
+                at(32.529 if rt == 6 else last + 0.01, weigh_z, rt, ("z", rt, 0), halves[0], False)
+                at(last + late + 0.141 + 0.819, weigh_z, rt, ("z", rt, 1), halves[1], False)
+            for rt in range(6):
+                at(28.092 + 1.249 * rt, weigh_z, rt, ("z", rt), slice(0, T), rt % 2 == 1 and rt / 6 < 0.829)
             for h in range(2):
-                interleave_d(1, 1, h, 2)
-            for h in range(2):
-                quantize_d(1, 1, h, 2)
-            for i in range(4):
-                score(1, i, 0, bank_b[i])
-            for i in range(8):
-                score(1, i, 1)
-                if i + 4 < 8:
-                    score(1, i + 4, 0, bank_b[i + 4])
-                emit(1, i, i % 2 == 1)
+                d0_due = 28.092 + 4 * 1.249 + 1.108 + 0.3 * h
+                at(d0_due, interleave_d, 0, halves[h])
+                at(d0_due + 0.919, quantize_d, 0, halves[h])
+                d1_due = last + 0.02 if h == 0 else last + 0.855 + 0.141 + 0.819 + 0.02
+                for k in range(2):
+                    docs = slice(h * HALF + k * P, h * HALF + (k + 1) * P)
+                    at(d1_due + 0.001 * k, interleave_d, 1, docs)
+                    at(d1_due + 0.0015 + 0.001 * k, quantize_d, 1, docs)
+            for i in range(16):
+                h = i // 8
+                due = last + (2.953, 10.096)[h] + 0.866 * (i % 8)
+                at(due - (0.336, 0.082)[h] * (i % 8 < 4), score, i, 0)
+                at(due + 0.001, score, i, 1)
+                at(due + 1.459, emit, i, i % 2 == 1)
+            for due, order, call, args in sorted(work, key=lambda item: item[:2]):
+                call(*args)

@@ -38,8 +38,8 @@ def tile_latent_term_projection_d4_kernel(
 
         ident = keep.tile([P, P], F32, name="ident")
         scale = keep.tile([P, GROUPS, PACK, V // BLK], F32, name="scale")
-        tw = keep.tile([P, PASSES, PACK], BF16, name="tw")
-        dw16 = keep.tile([P, GROUPS, PACK], BF16, name="dw16")
+        packed = keep.tile([P, K_PASS], BF16, name="packed")
+        factors = keep.tile([P, PASSES + GROUPS, PACK], BF16, name="factors")
         dw = keep.tile([P, GROUPS, PACK], F32, name="dw")
         a_codes = keep.tile([P, PASSES, T], U32, name="a_codes", align_bytes=64)
         a_planes = keep.tile([P, PASSES, T], U8, name="a_planes", align_bytes=64)
@@ -64,9 +64,11 @@ def tile_latent_term_projection_d4_kernel(
 
         raw = {}
 
-        def load_counts(g):
+        def load_counts(g, parts=1):
             raw[g] = flow.tile([P, PACK, T], BF16, name="raw", tag="raw", bufs=8)
-            nc.sync.dma_start(out=raw[g][:], in_=counts_view[g])
+            for k in range(parts):
+                js = slice(k * PACK // parts, (k + 1) * PACK // parts)
+                nc.sync.dma_start(out=raw[g][:, js, :], in_=counts_view[g, :, js, :])
 
         free_banks = ["b%d" % i for i in range(8)]
         held = {}
@@ -93,7 +95,7 @@ def tile_latent_term_projection_d4_kernel(
             nc.vector.tensor_tensor(
                 out=a_bf[g][:, docs, :].rearrange("p (c i) j -> p c j i", i=4),
                 in0=logs[g][:, :, docs].rearrange("p j (c i) -> p c j i", i=4),
-                in1=tw[:, g, :].unsqueeze(1).unsqueeze(3).to_broadcast([P, HALF // 4, PACK, 4]),
+                in1=factors[:, g, :].unsqueeze(1).unsqueeze(3).to_broadcast([P, HALF // 4, PACK, 4]),
                 op=MULT,
             )
 
@@ -240,15 +242,17 @@ def tile_latent_term_projection_d4_kernel(
             nc.sync.dma_start(out=out[dt * P : (dt + 1) * P, cc * 512 : (cc + 1) * 512], in_=o_sb[:])
 
         with tc.manual_schedule():
-            nc.sync.dma_start(out=scale[:], in_=basis_scale.rearrange("(g m j) b -> m g j b", g=GROUPS, j=PACK))
-            load_bytes(0, 0, 4, 0, 512)
-            load_counts(0)
-            nc.scalar.dma_start(out=tw[:], in_=term_weight.rearrange("(g p j) -> p g j", p=P, j=PACK))
+            nc.vector.memset(packed[:], 0.0)
+            load_bytes(0, 0, 2, 0, 512)
+            nc.scalar.dma_start(out=packed[0:PASSES, :], in_=term_weight.rearrange("(g n) -> g n", g=PASSES))
+            nc.scalar.dma_start(out=packed[PASSES : PASSES + GROUPS, :], in_=dir_weight.rearrange("(g n) -> g n", g=GROUPS))
+            nc.scalar.dma_start(out=scale[:], in_=basis_scale.rearrange("(g m j) b -> m g j b", g=GROUPS, j=PACK))
+            load_counts(0, 2)
+            load_bytes(0, 2, 4, 0, 512)
             load_bytes(1, 0, 2, 0, 512)
             load_counts(1)
             load_bytes(0, 0, 4, 512, 1024)
             load_bytes(1, 0, 2, 512, 1024)
-            nc.scalar.dma_start(out=dw16[:], in_=dir_weight.rearrange("(g m j) -> m g j", g=GROUPS, j=PACK))
             load_counts(2)
             for k0 in range(1024, V, 1024):
                 load_bytes(0, 0, 4, k0, k0 + 1024)
@@ -270,6 +274,18 @@ def tile_latent_term_projection_d4_kernel(
                     in_=cat_scales[:, 4 * quad : 4 * quad + 4, :].bitcast(I32).rearrange("g q n -> q g n"),
                 )
             make_identity(nc, ident[:])
+            flipped = take([P, 2, P], "flipped")
+            words = packed[:].bitcast(F32)
+            for u in range(2):
+                nc.tensor.transpose(flipped[:, u, :], words[:, u : K_PASS // 2 : 2], ident[:])
+
+            def spread_factors():
+                nc.vector.tensor_copy(
+                    out=factors[:].rearrange("p g j -> p (g j)").bitcast(F32).rearrange("p (g u) -> p g u", u=2),
+                    in_=flipped[:, :, 0 : PASSES + GROUPS].rearrange("p u g -> p g u"),
+                )
+                give("flipped")
+
 
             work = []
 
@@ -277,51 +293,52 @@ def tile_latent_term_projection_d4_kernel(
                 work.append((due, len(work), call, args))
 
             def step(n):
-                return float(n) if n < 24 else 24 + (n - 24) * 0.821
+                return float(n) if n < 24 else 24 + (n - 24) * 0.797
 
             by_s, by_v = 0.5, 0.3
             for n in range(len(units)):
-                by_s += 0.603 if n < 24 else 0.852
-                by_v += 0 if n < 24 else 0.174
+                by_s += 0.649 if n < 24 else 0.475
+                by_v += 0 if n < 24 else 0.036
                 s_half = by_s >= 1 and n > 0
                 v_copy = by_v >= 1
                 by_s -= s_half
                 by_v -= v_copy
                 for h in range(2):
-                    at(step(n) - 0.671 + 0.02 * h, widen, n, h, s_half and h == 1)
+                    at(step(n) - 1.143 + 0.02 * h, widen, n, h, s_half and h == 1)
                 at(step(n), turn, n)
-                at(step(n) + 1.359, collect, n, v_copy)
-                at(step(n) + 1.359 + 2.921, quantize_b, n)
-                at(step(n) + 1.359 + 2.921 + 1.512, multiply_unit, n)
-            at(20.0, nc.vector.tensor_copy, dw[:], dw16[:])
+                at(step(n) + 1.461, collect, n, v_copy)
+                at(step(n) + 1.461 + 2.097, quantize_b, n)
+                at(step(n) + 1.461 + 2.097 + 1.331, multiply_unit, n)
+            at(0.4, spread_factors)
+            at(20.0, nc.vector.tensor_copy, dw[:], factors[:, PASSES:, :])
             for g in range(PASSES):
                 for k in range(2):
-                    at(3 * g - 1.081 + 0.281 * k, ln_part, g, k)
-                    at(3 * g - 1.081 + 2.706 + 1.364 * k, weigh_part, g, k)
-                at(3 * g - 1.081 + 2.706 + 1.364 + 1.171, quantize_a, g)
-            last = step(31) + 1.359 + 2.921 + 1.512
+                    at(3 * g - 2.645 + 1.376 * k, ln_part, g, k)
+                    at(3 * g - 2.645 + 3.783 + 0.525 * k, weigh_part, g, k)
+                at(3 * g - 2.645 + 3.783 + 0.525 + 1.641, quantize_a, g)
+            last = step(31) + 1.461 + 2.097 + 1.331
             halves = (slice(0, HALF), slice(HALF, T))
-            for rt, late in ((6, 0.601), (7, 0.855)):
+            for rt, late in ((6, 3.409), (7, 3.69)):
                 at(last + late, multiply_late, rt, range(4))
-                at(last + late + 0.141, multiply_late, rt, range(4, 8))
-                at(32.529 if rt == 6 else last + 0.01, weigh_z, rt, ("z", rt, 0), halves[0], False)
-                at(last + late + 0.141 + 0.819, weigh_z, rt, ("z", rt, 1), halves[1], False)
+                at(last + late + 0.643, multiply_late, rt, range(4, 8))
+                at(32.038 if rt == 6 else last + 0.01, weigh_z, rt, ("z", rt, 0), halves[0], False)
+                at(last + late + 0.643 + 3.589, weigh_z, rt, ("z", rt, 1), halves[1], False)
             for rt in range(6):
-                at(28.092 + 1.249 * rt, weigh_z, rt, ("z", rt), slice(0, T), rt % 2 == 1 and rt / 6 < 0.829)
+                at(27.705 + 1.301 * rt, weigh_z, rt, ("z", rt), slice(0, T), rt % 2 == 1 and rt / 6 < 0.059)
             for h in range(2):
-                d0_due = 28.092 + 4 * 1.249 + 1.108 + 0.3 * h
+                d0_due = 27.705 + 4 * 1.301 + 0.572 + 0.3 * h
                 at(d0_due, interleave_d, 0, halves[h])
-                at(d0_due + 0.919, quantize_d, 0, halves[h])
-                d1_due = last + 0.02 if h == 0 else last + 0.855 + 0.141 + 0.819 + 0.02
+                at(d0_due + 0.993, quantize_d, 0, halves[h])
+                d1_due = last + 0.02 if h == 0 else last + 3.69 + 0.643 + 3.589 + 0.02
                 for k in range(2):
                     docs = slice(h * HALF + k * P, h * HALF + (k + 1) * P)
                     at(d1_due + 0.001 * k, interleave_d, 1, docs)
                     at(d1_due + 0.0015 + 0.001 * k, quantize_d, 1, docs)
             for i in range(16):
                 h = i // 8
-                due = last + (2.953, 10.096)[h] + 0.866 * (i % 8)
-                at(due - (0.336, 0.082)[h] * (i % 8 < 4), score, i, 0)
+                due = last + (10.61, 22.192)[h] + 1.62 * (i % 8)
+                at(due - (0.002, 1.332)[h] * (i % 8 < 4), score, i, 0)
                 at(due + 0.001, score, i, 1)
-                at(due + 1.459, emit, i, i % 2 == 1)
+                at(due + 3.323, emit, i, i % 2 == 1)
             for due, order, call, args in sorted(work, key=lambda item: item[:2]):
                 call(*args)

@@ -3,8 +3,8 @@ from contextlib import ExitStack
 import concourse.mybir as mybir
 from concourse.masks import make_identity
 
-V, T, R, C = 4096, 512, 1024, 2048
-FLOPS = 2 * V * T * R + 2 * T * R * C
+TERMS, DOCS, DIRECTIONS, CATEGORIES = 4096, 512, 1024, 2048
+FLOPS = 2 * TERMS * DOCS * DIRECTIONS + 2 * DOCS * DIRECTIONS * CATEGORIES
 
 F32 = mybir.dt.float32
 BF16 = mybir.dt.bfloat16
@@ -15,16 +15,23 @@ FP8 = mybir.dt.float8_e4m3fn
 E4M3 = mybir.dt.float8_e4m3fn_x4
 E2M1 = mybir.dt.float4_e2m1fn_x4
 MULT = mybir.AluOpType.mult
-ACT = mybir.ActivationFunctionType
+COPY = mybir.ActivationFunctionType.Copy
+LN = mybir.ActivationFunctionType.Ln
 
 P = 128
 PACK = 4
 K_PASS = P * PACK
-PASSES = V // K_PASS
-BLK = 128
-BLOCKS = K_PASS // BLK
-GROUPS = R // K_PASS
-HALF = T // 2
+PASSES = TERMS // K_PASS
+GROUPS = DIRECTIONS // K_PASS
+SCALE_RUN = 128
+RUNS = K_PASS // SCALE_RUN
+HALF = DOCS // 2
+N_TILE = 512
+BANKS = 8
+
+ROW_TILES = DIRECTIONS // P
+VECTOR_WEIGHS = (3, 5)
+EARLY = 6
 
 
 def tile_latent_term_projection_d4_kernel(
@@ -37,308 +44,338 @@ def tile_latent_term_projection_d4_kernel(
         psum = ctx.enter_context(tc.psum_pool(name="psum", bufs=1))
 
         ident = keep.tile([P, P], F32, name="ident")
-        scale = keep.tile([P, GROUPS, PACK, V // BLK], F32, name="scale")
-        packed = keep.tile([P, K_PASS], BF16, name="packed")
-        factors = keep.tile([P, PASSES + GROUPS, PACK], BF16, name="factors")
-        dw = keep.tile([P, GROUPS, PACK], F32, name="dw")
-        a_codes = keep.tile([P, PASSES, T], U32, name="a_codes", align_bytes=64)
-        a_planes = keep.tile([P, PASSES, T], U8, name="a_planes", align_bytes=64)
-        b_codes = keep.tile([P, 32, 256], U32, name="b_codes", align_bytes=64)
-        b_planes = keep.tile([P, 32, 256], U8, name="b_planes", align_bytes=64)
-        d_codes = keep.tile([P, GROUPS, T], U32, name="d_codes", align_bytes=64)
-        d_planes = keep.tile([P, GROUPS, T], U8, name="d_planes", align_bytes=64)
-        cat = keep.tile([P, GROUPS, 2 * C], U8, name="cat", align_bytes=64)
-        cat_planes = keep.tile([P, GROUPS, C], U8, name="cat_planes", align_bytes=64)
+        scale = keep.tile([P, GROUPS, PACK, TERMS // SCALE_RUN], F32, name="scale")
+        weight_rows = keep.tile([P, K_PASS], BF16, name="weight_rows")
+        weights = keep.tile([P, PASSES + GROUPS, PACK], BF16, name="weights")
+        dir_factor = keep.tile([P, GROUPS, PACK], F32, name="dir_factor")
+        a_codes = keep.tile([P, PASSES, DOCS], U32, name="a_codes", align_bytes=64)
+        a_scales = keep.tile([P, PASSES, DOCS], U8, name="a_scales", align_bytes=64)
+        d_codes = keep.tile([P, GROUPS, DOCS], U32, name="d_codes", align_bytes=64)
+        d_scales = keep.tile([P, GROUPS, DOCS], U8, name="d_scales", align_bytes=64)
+        d_planes = [keep.tile([P, PACK, DOCS], BF16, name="d_planes%d" % gr) for gr in range(GROUPS)]
+        d_words = [keep.tile([P, DOCS, PACK], BF16, name="d_words%d" % gr, align_bytes=64) for gr in range(GROUPS)]
+        cat = keep.tile([P, GROUPS, 2 * CATEGORIES], U8, name="cat", align_bytes=64)
+        cat_planes = keep.tile([P, GROUPS, CATEGORIES], U8, name="cat_planes", align_bytes=64)
 
-        bytes_view = basis_bytes.rearrange("(g m j) k -> g m j k", g=GROUPS, j=PACK)
-        counts_view = counts.rearrange("(g p j) w -> g p j w", p=P, j=PACK)
+        units = [((rt, g), (rt + 1, g)) for g in range(PASSES) for rt in range(0, EARLY, 2)]
+        n_early = len(units)
+        units += [((rt, g), (rt, g + 1)) for rt in range(EARLY, ROW_TILES) for g in range(0, PASSES, 2)]
+        place = {tile_of: (n, h) for n, unit in enumerate(units) for h, tile_of in enumerate(unit)}
+        b_codes = keep.tile([P, len(units), 2 * P], U32, name="b_codes", align_bytes=64)
+        b_scales = keep.tile([P, len(units), 2 * P], U8, name="b_scales", align_bytes=64)
 
-        byt = {}
+        free_banks = ["bank%d" % i for i in range(BANKS)]
+        bank_of = {}
+
+        def take_bank(key, shape):
+            bank_of[key] = free_banks.pop(0)
+            return psum.tile(shape, F32, name="psum_tile", tag=bank_of[key])
+
+        def give_bank(key):
+            free_banks.append(bank_of[key])
+
+        byte_run, raw = {}, {}
+        bytes_view = basis_bytes.rearrange("(gr m j) k -> gr m j k", gr=GROUPS, j=PACK)
+        counts_view = counts.rearrange("(g p t) w -> g p t w", p=P, t=PACK)
 
         def load_bytes(gr, j0, j1, k0, k1):
-            held = keep.tile([P, j1 - j0, k1 - k0], U8, name="byt_%d_%d_%d" % (gr, j0, k0))
+            held = keep.tile([P, j1 - j0, k1 - k0], U8, name="bytes_%d_%d_%d" % (gr, j0, k0))
             nc.sync.dma_start(out=held[:], in_=bytes_view[gr, :, j0:j1, k0:k1])
             for j in range(j0, j1):
-                for b in range(k0 // BLK, k1 // BLK):
-                    byt[(gr, j, b)] = held[:, j - j0, b * BLK - k0 : (b + 1) * BLK - k0]
-
-        raw = {}
+                for k in range(k0, k1, SCALE_RUN):
+                    byte_run[(PACK * gr + j, k // SCALE_RUN)] = held[:, j - j0, k - k0 : k - k0 + SCALE_RUN]
 
         def load_counts(g, parts=1):
-            raw[g] = flow.tile([P, PACK, T], BF16, name="raw", tag="raw", bufs=8)
-            for k in range(parts):
-                js = slice(k * PACK // parts, (k + 1) * PACK // parts)
-                nc.sync.dma_start(out=raw[g][:, js, :], in_=counts_view[g, :, js, :])
+            raw[g] = flow.tile([P, PACK, DOCS], BF16, name="raw", tag="stream", bufs=PASSES)
+            for i in range(parts):
+                rows = slice(i * PACK // parts, (i + 1) * PACK // parts)
+                nc.sync.dma_start(out=raw[g][:, rows, :], in_=counts_view[g, :, rows, :])
 
-        free_banks = ["b%d" % i for i in range(8)]
-        held = {}
+        logs, a_words = {}, {}
 
-        def take(shape, key):
-            held[key] = free_banks.pop(0)
-            return psum.tile(shape, F32, name="bank", tag=held[key])
+        def take_log(g, i):
+            if i == 0:
+                logs[g] = flow.tile([P, PACK, DOCS], F32, name="logs", tag="logs", bufs=3)
+            rows = slice(2 * i, 2 * i + 2)
+            nc.scalar.activation(out=logs[g][:, rows, :], in_=raw[g][:, rows, :], func=LN, bias=1.0, scale=1.0)
 
-        def give(key):
-            free_banks.append(held[key])
-
-        logs, a_bf = {}, {}
-
-        def ln_part(g, k):
-            if k == 0:
-                logs[g] = flow.tile([P, PACK, T], F32, name="logs", tag="logs", bufs=3)
-            js = slice(2 * k, 2 * k + 2)
-            nc.scalar.activation(out=logs[g][:, js, :], in_=raw[g][:, js, :], func=ACT.Ln, bias=1.0, scale=1.0)
-
-        def weigh_part(g, k):
-            if k == 0:
-                a_bf[g] = flow.tile([P, T, PACK], BF16, name="a_bf", tag="a_bf", bufs=3, align_bytes=64)
-            docs = slice(k * HALF, (k + 1) * HALF)
+        def weigh_terms(g, i):
+            if i == 0:
+                a_words[g] = flow.tile([P, DOCS, PACK], BF16, name="a_words", tag="a_words", bufs=3, align_bytes=64)
+            docs = slice(i * HALF, (i + 1) * HALF)
             nc.vector.tensor_tensor(
-                out=a_bf[g][:, docs, :].rearrange("p (c i) j -> p c j i", i=4),
-                in0=logs[g][:, :, docs].rearrange("p j (c i) -> p c j i", i=4),
-                in1=factors[:, g, :].unsqueeze(1).unsqueeze(3).to_broadcast([P, HALF // 4, PACK, 4]),
+                out=a_words[g][:, docs, :].rearrange("p (c i) t -> p c t i", i=4),
+                in0=logs[g][:, :, docs].rearrange("p t (c i) -> p c t i", i=4),
+                in1=weights[:, g, :].unsqueeze(1).unsqueeze(3).to_broadcast([P, HALF // 4, PACK, 4]),
                 op=MULT,
             )
 
         def quantize_a(g):
             nc.vector.quantize_mx(
                 out=a_codes[:, g, :].bitcast(E4M3),
-                scales=a_planes[:, g, :],
-                in_=a_bf[g][:].rearrange("p w j -> p (w j)"),
+                scales=a_scales[:, g, :],
+                in_=a_words[g][:].rearrange("p w t -> p (w t)"),
             )
 
-        units = [((2 * i, g), (2 * i + 1, g)) for g in range(PASSES) for i in range(3)]
-        units += [((rt, 2 * i), (rt, 2 * i + 1)) for rt in (6, 7) for i in range(4)]
-        home = {}
-        for n, unit in enumerate(units):
-            for h, tile_of in enumerate(unit):
-                home[tile_of] = (n, h)
-        wide, turned, grouped, by_scalar = {}, {}, {}, {}
+        wide, turned, grouped = {}, {}, {}
 
-        def widen(n, h, on_scalar):
-            if h == 0:
-                wide[n] = flow.tile([P, 2, K_PASS], BF16, name="wide", tag="wide", bufs=4)
-            by_scalar[(n, h)] = on_scalar
-            rt, g = units[n][h]
-            gr, j = divmod(rt, PACK)
-            by_word = wide[n][:, h, :].rearrange("p (u w e) -> p w u e", u=2, e=2)
-            for q in range(BLOCKS):
-                b = BLOCKS * g + q
-                src = byt[(gr, j, b)].bitcast(FP8)
-                factor = scale[:, gr, j, b : b + 1]
-                if on_scalar:
-                    nc.scalar.activation(out=wide[n][:, h, q * BLK : (q + 1) * BLK], in_=src, func=ACT.Copy, scale=factor)
-                else:
-                    nc.vector.tensor_scalar(
-                        out=by_word[:, 32 * q : 32 * q + 32, :, :],
-                        in0=src.rearrange("p (w u e) -> p w u e", u=2, e=2),
-                        scalar1=factor,
-                        scalar2=None,
-                        op0=MULT,
-                    )
+        def on_scalar(n, h):
+            if n < n_early:
+                return h == 1 and n % 3 != 0
+            return h == 1 and n % 2 == 1 and n < len(units) - 2
+
+        def widen(n):
+            wide[n] = flow.tile([P, 2, K_PASS], BF16, name="wide", tag="wide", bufs=4)
+            for h, (rt, g) in enumerate(units[n]):
+                gr, j = divmod(rt, PACK)
+                by_parity = wide[n][:, h, :].rearrange("p (u w e) -> p w u e", u=2, e=2)
+                for q in range(RUNS):
+                    run = RUNS * g + q
+                    values = byte_run[(rt, run)].bitcast(FP8)
+                    factor = scale[:, gr, j, run : run + 1]
+                    if on_scalar(n, h):
+                        terms = slice(q * SCALE_RUN, (q + 1) * SCALE_RUN)
+                        nc.scalar.activation(out=wide[n][:, h, terms], in_=values, func=COPY, scale=factor)
+                    else:
+                        word_pairs = slice(q * SCALE_RUN // 4, (q + 1) * SCALE_RUN // 4)
+                        nc.vector.tensor_scalar(
+                            out=by_parity[:, word_pairs, :, :],
+                            in0=values.rearrange("p (w u e) -> p w u e", u=2, e=2),
+                            scalar1=factor,
+                            scalar2=None,
+                            op0=MULT,
+                        )
 
         def turn(n):
-            turned[n] = take([P, 2, 2, P], ("turned", n))
+            turned[n] = take_bank(("turned", n), [P, 2, 2, P])
             for h in range(2):
                 words = wide[n][:, h, :].bitcast(F32)
                 for u in range(2):
-                    picked = words[:, u : 2 * P : 2] if by_scalar[(n, h)] else words[:, u * P : (u + 1) * P]
+                    picked = words[:, u : 2 * P : 2] if on_scalar(n, h) else words[:, u * P : (u + 1) * P]
                     nc.tensor.transpose(turned[n][:, h, u, :], picked, ident[:])
 
-        def collect(n, on_vector):
+        def collect(n):
             grouped[n] = flow.tile([P, 2, P, PACK], BF16, name="grouped", tag="grouped", bufs=6, align_bytes=64)
-            dst = grouped[n][:].rearrange("p h r j -> p (h r j)").bitcast(F32).rearrange("p (h r u) -> p h r u", h=2, u=2)
-            src = turned[n][:].rearrange("p h u r -> p h r u")
-            if on_vector:
-                nc.vector.tensor_copy(out=dst, in_=src)
-            else:
-                nc.scalar.copy(out=dst, in_=src)
-            give(("turned", n))
+            words = grouped[n][:].rearrange("p h r t -> p (h r t)").bitcast(F32)
+            nc.scalar.copy(
+                out=words.rearrange("p (h r u) -> p h r u", h=2, u=2), in_=turned[n][:].rearrange("p h u r -> p h r u")
+            )
+            give_bank(("turned", n))
 
         def quantize_b(n):
             nc.vector.quantize_mx(
                 out=b_codes[:, n, :].bitcast(E4M3),
-                scales=b_planes[:, n, :],
-                in_=grouped[n][:].rearrange("p h r j -> p (h r j)"),
+                scales=b_scales[:, n, :],
+                in_=grouped[n][:].rearrange("p h r t -> p (h r t)"),
             )
 
         z = {}
 
-        def multiply(rt, g, key, docs):
-            at, h = home[(rt, g)]
+        def multiply(rt, g, docs):
+            n, h = place[(rt, g)]
             cols = slice(h * P, (h + 1) * P)
+            key = (rt, docs.start)
             if g == 0:
-                z[key] = take([P, docs.stop - docs.start], key)
+                z[key] = take_bank(key, [P, docs.stop - docs.start])
             nc.tensor.matmul_mx(
                 out=z[key][:],
-                lhsT=b_codes[:, at, cols].bitcast(E4M3),
-                lhsT_scale=b_planes[:, at, cols],
+                lhsT=b_codes[:, n, cols].bitcast(E4M3),
+                lhsT_scale=b_scales[:, n, cols],
                 rhs=a_codes[:, g, docs].bitcast(E4M3),
-                rhs_scale=a_planes[:, g, docs],
+                rhs_scale=a_scales[:, g, docs],
                 start=(g == 0),
                 stop=(g == PASSES - 1),
             )
 
+        all_docs, first_docs, second_docs = slice(0, DOCS), slice(0, HALF), slice(HALF, DOCS)
+
         def multiply_unit(n):
             for rt, g in units[n]:
-                if rt < 6:
-                    multiply(rt, g, ("z", rt), slice(0, T))
-                else:
-                    multiply(rt, g, ("z", rt, 0), slice(0, HALF))
+                multiply(rt, g, all_docs if rt < EARLY else first_docs)
 
-        def multiply_late(rt, passes):
-            for g in passes:
-                multiply(rt, g, ("z", rt, 1), slice(HALF, T))
-
-        dz = [keep.tile([P, PACK, T], BF16, name="dz%d" % gr) for gr in range(GROUPS)]
-        d_bf = [keep.tile([P, T, PACK], BF16, name="d_bf%d" % gr, align_bytes=64) for gr in range(GROUPS)]
-
-        def weigh_z(rt, key, docs, on_vector):
+        def weigh_directions(rt, docs):
             gr, j = divmod(rt, PACK)
-            dst = dz[gr][:, j, docs]
-            if on_vector:
-                nc.vector.tensor_scalar(out=dst, in0=z[key][:], scalar1=dw[:, gr, j : j + 1], scalar2=None, op0=MULT)
+            key = (rt, docs.start)
+            plane = d_planes[gr][:, j, docs]
+            factor = dir_factor[:, gr, j : j + 1]
+            if rt in VECTOR_WEIGHS:
+                nc.vector.tensor_scalar(out=plane, in0=z[key][:], scalar1=factor, scalar2=None, op0=MULT)
             else:
-                nc.scalar.activation(out=dst, in_=z[key][:], func=ACT.Copy, scale=dw[:, gr, j : j + 1])
-            give(key)
+                nc.scalar.activation(out=plane, in_=z[key][:], func=COPY, scale=factor)
+            give_bank(key)
 
         def interleave_d(gr, docs):
             nc.vector.tensor_copy(
-                out=d_bf[gr][:, docs, :].rearrange("p (c i) j -> p c j i", i=4),
-                in_=dz[gr][:, :, docs].rearrange("p j (c i) -> p c j i", i=4),
+                out=d_words[gr][:, docs, :].rearrange("p (c i) j -> p c j i", i=4),
+                in_=d_planes[gr][:, :, docs].rearrange("p j (c i) -> p c j i", i=4),
             )
 
         def quantize_d(gr, docs):
             nc.vector.quantize_mx(
                 out=d_codes[:, gr, docs].bitcast(E4M3),
-                scales=d_planes[:, gr, docs],
-                in_=d_bf[gr][:, docs, :].rearrange("p w j -> p (w j)"),
+                scales=d_scales[:, gr, docs],
+                in_=d_words[gr][:, docs, :].rearrange("p w j -> p (w j)"),
             )
 
-        o = {}
+        results = {}
 
-        def score(i, gr):
-            dt, cc = divmod(i, 4)
-            if gr == 0:
-                o[i] = take([P, 512], ("o", i))
-            docs = slice(dt * P, (dt + 1) * P)
-            nc.tensor.matmul_mx(
-                out=o[i][:],
-                lhsT=d_codes[:, gr, docs].bitcast(E4M3),
-                lhsT_scale=d_planes[:, gr, docs],
-                rhs=cat[:, gr, cc * 1024 : (cc + 1) * 1024].bitcast(E2M1),
-                rhs_scale=cat_planes[:, gr, cc * 512 : (cc + 1) * 512],
-                start=(gr == 0),
-                stop=(gr == 1),
-            )
-
-        def emit(i, on_vector):
-            dt, cc = divmod(i, 4)
-            o_sb = flow.tile([P, 512], F32, name="o_sb", tag="raw", bufs=8)
-            if on_vector:
-                nc.vector.tensor_copy(out=o_sb[:], in_=o[i][:])
+        def score(i):
+            row_tile, col_tile = divmod(i, CATEGORIES // N_TILE)
+            rows = slice(row_tile * P, (row_tile + 1) * P)
+            cols = slice(col_tile * N_TILE, (col_tile + 1) * N_TILE)
+            acc = take_bank(("score", i), [P, N_TILE])
+            for gr in range(GROUPS):
+                nc.tensor.matmul_mx(
+                    out=acc[:],
+                    lhsT=d_codes[:, gr, rows].bitcast(E4M3),
+                    lhsT_scale=d_scales[:, gr, rows],
+                    rhs=cat[:, gr, 2 * cols.start : 2 * cols.stop].bitcast(E2M1),
+                    rhs_scale=cat_planes[:, gr, cols],
+                    start=(gr == 0),
+                    stop=(gr == GROUPS - 1),
+                )
+            if i % 2 == 0:
+                results[i // 2] = flow.tile([P, 2, N_TILE], F32, name="results", tag="stream", bufs=PASSES)
+            result = results[i // 2][:, i % 2, :]
+            if i % 2 == 0:
+                nc.scalar.copy(out=result, in_=acc[:])
             else:
-                nc.scalar.copy(out=o_sb[:], in_=o[i][:])
-            give(("o", i))
-            nc.sync.dma_start(out=out[dt * P : (dt + 1) * P, cc * 512 : (cc + 1) * 512], in_=o_sb[:])
+                nc.vector.tensor_copy(out=result, in_=acc[:])
+            give_bank(("score", i))
+            nc.sync.dma_start(out=out[rows, cols], in_=result)
 
         with tc.manual_schedule():
-            nc.vector.memset(packed[:], 0.0)
-            load_bytes(0, 0, 2, 0, 512)
-            nc.scalar.dma_start(out=packed[0:PASSES, :], in_=term_weight.rearrange("(g n) -> g n", g=PASSES))
-            nc.scalar.dma_start(out=packed[PASSES : PASSES + GROUPS, :], in_=dir_weight.rearrange("(g n) -> g n", g=GROUPS))
+            nc.vector.memset(weight_rows[:], 0.0)
+            load_bytes(0, 0, 2, 0, K_PASS)
+            nc.scalar.dma_start(out=weight_rows[0:PASSES, :], in_=term_weight.rearrange("(g n) -> g n", g=PASSES))
+            nc.scalar.dma_start(
+                out=weight_rows[PASSES : PASSES + GROUPS, :], in_=dir_weight.rearrange("(g n) -> g n", g=GROUPS)
+            )
             nc.scalar.dma_start(out=scale[:], in_=basis_scale.rearrange("(g m j) b -> m g j b", g=GROUPS, j=PACK))
-            load_counts(0, 2)
-            load_bytes(0, 2, 4, 0, 512)
-            load_bytes(1, 0, 2, 0, 512)
+            load_counts(0, parts=2)
+            load_bytes(0, 2, 4, 0, K_PASS)
+            load_bytes(1, 0, 2, 0, K_PASS)
             load_counts(1)
-            load_bytes(0, 0, 4, 512, 1024)
-            load_bytes(1, 0, 2, 512, 1024)
+            load_bytes(0, 0, 4, K_PASS, 2 * K_PASS)
+            load_bytes(1, 0, 2, K_PASS, 2 * K_PASS)
             load_counts(2)
-            for k0 in range(1024, V, 1024):
-                load_bytes(0, 0, 4, k0, k0 + 1024)
-                load_bytes(1, 0, 2, k0, k0 + 1024)
-                load_counts(k0 // 512 + 1)
-                if k0 // 512 + 2 < PASSES:
-                    load_counts(k0 // 512 + 2)
-            for k0 in range(0, V, 2048):
-                load_bytes(1, 2, 4, k0, k0 + 2048)
+            for g in range(2, PASSES, 2):
+                load_bytes(0, 0, 4, g * K_PASS, (g + 2) * K_PASS)
+                load_bytes(1, 0, 2, g * K_PASS, (g + 2) * K_PASS)
+                for later in range(g + 1, min(g + 3, PASSES)):
+                    load_counts(later)
+            for k0 in (0, TERMS // 2):
+                load_bytes(1, 2, 4, k0, k0 + TERMS // 2)
             nc.sync.dma_start(
                 out=cat[:].rearrange("p g n -> p (g n)").bitcast(I32).rearrange("p (g n) -> p g n", g=GROUPS),
                 in_=cat_words.bitcast(I32).rearrange("g p n -> p g n"),
             )
-            planes_i32 = cat_planes[:].rearrange("p g n -> p (g n)").bitcast(I32)
-            nc.vector.memset(planes_i32, 0)
-            for quad in range(4):
+            scale_words = cat_planes[:].rearrange("p g n -> p (g n)").bitcast(I32)
+            nc.vector.memset(scale_words, 0)
+            for quadrant in range(4):
                 nc.sync.dma_start(
-                    out=planes_i32[32 * quad : 32 * quad + 4, :].rearrange("p (g n) -> p g n", g=GROUPS),
-                    in_=cat_scales[:, 4 * quad : 4 * quad + 4, :].bitcast(I32).rearrange("g q n -> q g n"),
+                    out=scale_words[32 * quadrant : 32 * quadrant + 4, :].rearrange("p (g n) -> p g n", g=GROUPS),
+                    in_=cat_scales[:, 4 * quadrant : 4 * quadrant + 4, :].bitcast(I32).rearrange("g q n -> q g n"),
                 )
             make_identity(nc, ident[:])
-            flipped = take([P, 2, P], "flipped")
-            words = packed[:].bitcast(F32)
+
+            row_words = weight_rows[:].bitcast(F32)
+            turned_rows = take_bank("turned_rows", [P, 2, P])
             for u in range(2):
-                nc.tensor.transpose(flipped[:, u, :], words[:, u : K_PASS // 2 : 2], ident[:])
+                nc.tensor.transpose(turned_rows[:, u, :], row_words[:, u : 2 * P : 2], ident[:])
 
-            def spread_factors():
-                nc.vector.tensor_copy(
-                    out=factors[:].rearrange("p g j -> p (g j)").bitcast(F32).rearrange("p (g u) -> p g u", u=2),
-                    in_=flipped[:, :, 0 : PASSES + GROUPS].rearrange("p u g -> p g u"),
-                )
-                give("flipped")
+            widen(0)
+            take_log(0, 0)
+            take_log(0, 1)
+            widen(1)
+            nc.vector.tensor_copy(
+                out=weights[:].rearrange("p g t -> p (g t)").bitcast(F32).rearrange("p (g u) -> p g u", u=2),
+                in_=turned_rows[:, :, 0 : PASSES + GROUPS].rearrange("p u g -> p g u"),
+            )
+            give_bank("turned_rows")
+            for s in range(n_early):
+                g, third = divmod(s, 3)
+                turn(s)
+                if third == 1:
+                    weigh_terms(g, 0)
+                if third == 0 and g > 0:
+                    quantize_a(g - 1)
+                if third == 0 and g + 1 < PASSES:
+                    take_log(g + 1, 0)
+                if s >= 1:
+                    collect(s - 1)
+                if s >= 3:
+                    quantize_b(s - 3)
+                if third == 1:
+                    weigh_terms(g, 1)
+                if third == 1 and g + 1 < PASSES:
+                    take_log(g + 1, 1)
+                widen(s + 2)
+                if s >= 4:
+                    multiply_unit(s - 4)
+            quantize_a(PASSES - 1)
+            nc.vector.tensor_copy(out=dir_factor[:], in_=weights[:, PASSES:, :])
 
+            last = len(units) - 1
+            pause = last - 2
+            for s in range(n_early, len(units)):
+                turn(s)
+                if s + 2 <= last:
+                    widen(s + 2)
+                collect(s - 1)
+                if s in (n_early + 4, n_early + 5):
+                    weigh_directions(s - n_early - 4, all_docs)
+                quantize_b(s - 3)
+                if n_early < s < pause:
+                    multiply_unit(s - 5)
+                elif s > pause:
+                    multiply_unit(s - 6)
+            weigh_directions(2, all_docs)
+            collect(last)
+            quantize_b(last - 2)
+            weigh_directions(3, all_docs)
+            quantize_b(last - 1)
+            for n in range(last - 5, last - 1):
+                multiply_unit(n)
+            weigh_directions(6, first_docs)
+            weigh_directions(4, all_docs)
+            quantize_b(last)
+            weigh_directions(5, all_docs)
+            multiply_unit(last - 1)
+            multiply_unit(last)
+            weigh_directions(7, first_docs)
 
-            work = []
+            quarter = [slice(i * P, (i + 1) * P) for i in range(DOCS // P)]
+            interleave_d(0, quarter[0])
+            interleave_d(0, quarter[1])
+            quantize_d(0, quarter[0])
+            interleave_d(1, quarter[0])
+            quantize_d(0, quarter[1])
+            quantize_d(1, quarter[0])
+            interleave_d(1, quarter[1])
+            interleave_d(0, quarter[2])
+            quantize_d(1, quarter[1])
+            interleave_d(0, quarter[3])
 
-            def at(due, call, *args):
-                work.append((due, len(work), call, args))
-
-            def step(n):
-                return float(n) if n < 24 else 24 + (n - 24) * 0.797
-
-            by_s, by_v = 0.5, 0.3
-            for n in range(len(units)):
-                by_s += 0.649 if n < 24 else 0.475
-                by_v += 0 if n < 24 else 0.036
-                s_half = by_s >= 1 and n > 0
-                v_copy = by_v >= 1
-                by_s -= s_half
-                by_v -= v_copy
-                for h in range(2):
-                    at(step(n) - 1.143 + 0.02 * h, widen, n, h, s_half and h == 1)
-                at(step(n), turn, n)
-                at(step(n) + 1.461, collect, n, v_copy)
-                at(step(n) + 1.461 + 2.097, quantize_b, n)
-                at(step(n) + 1.461 + 2.097 + 1.331, multiply_unit, n)
-            at(0.4, spread_factors)
-            at(20.0, nc.vector.tensor_copy, dw[:], factors[:, PASSES:, :])
             for g in range(PASSES):
-                for k in range(2):
-                    at(3 * g - 2.645 + 1.376 * k, ln_part, g, k)
-                    at(3 * g - 2.645 + 3.783 + 0.525 * k, weigh_part, g, k)
-                at(3 * g - 2.645 + 3.783 + 0.525 + 1.641, quantize_a, g)
-            last = step(31) + 1.461 + 2.097 + 1.331
-            halves = (slice(0, HALF), slice(HALF, T))
-            for rt, late in ((6, 3.409), (7, 3.69)):
-                at(last + late, multiply_late, rt, range(4))
-                at(last + late + 0.643, multiply_late, rt, range(4, 8))
-                at(32.038 if rt == 6 else last + 0.01, weigh_z, rt, ("z", rt, 0), halves[0], False)
-                at(last + late + 0.643 + 3.589, weigh_z, rt, ("z", rt, 1), halves[1], False)
-            for rt in range(6):
-                at(27.705 + 1.301 * rt, weigh_z, rt, ("z", rt), slice(0, T), rt % 2 == 1 and rt / 6 < 0.059)
-            for h in range(2):
-                d0_due = 27.705 + 4 * 1.301 + 0.572 + 0.3 * h
-                at(d0_due, interleave_d, 0, halves[h])
-                at(d0_due + 0.993, quantize_d, 0, halves[h])
-                d1_due = last + 0.02 if h == 0 else last + 3.69 + 0.643 + 3.589 + 0.02
-                for k in range(2):
-                    docs = slice(h * HALF + k * P, h * HALF + (k + 1) * P)
-                    at(d1_due + 0.001 * k, interleave_d, 1, docs)
-                    at(d1_due + 0.0015 + 0.001 * k, quantize_d, 1, docs)
-            for i in range(16):
-                h = i // 8
-                due = last + (10.61, 22.192)[h] + 1.62 * (i % 8)
-                at(due - (0.002, 1.332)[h] * (i % 8 < 4), score, i, 0)
-                at(due + 0.001, score, i, 1)
-                at(due + 3.323, emit, i, i % 2 == 1)
-            for due, order, call, args in sorted(work, key=lambda item: item[:2]):
-                call(*args)
+                multiply(6, g, second_docs)
+            for g in range(PASSES // 2):
+                multiply(7, g, second_docs)
+            weigh_directions(6, second_docs)
+            for i in range(4):
+                score(i)
+            for g in range(PASSES // 2, PASSES):
+                multiply(7, g, second_docs)
+            for i in range(4, 6):
+                score(i)
+            weigh_directions(7, second_docs)
+            quantize_d(0, quarter[2])
+            quantize_d(0, quarter[3])
+            interleave_d(1, quarter[2])
+            quantize_d(1, quarter[2])
+            for i in range(6, 8):
+                score(i)
+            interleave_d(1, quarter[3])
+            quantize_d(1, quarter[3])
+            for i in range(8, (DOCS // P) * (CATEGORIES // N_TILE)):
+                score(i)

from contextlib import ExitStack

import concourse.mybir as mybir
from concourse.masks import make_identity

TERMS, DOCS, DIRECTIONS, CATEGORIES = 4096, 512, 1024, 2048
FLOPS = 2 * TERMS * DOCS * DIRECTIONS + 2 * DOCS * DIRECTIONS * CATEGORIES

F32 = mybir.dt.float32
BF16 = mybir.dt.bfloat16
U32 = mybir.dt.uint32
I32 = mybir.dt.int32
U8 = mybir.dt.uint8
FP8 = mybir.dt.float8_e4m3fn
E4M3 = mybir.dt.float8_e4m3fn_x4
E2M1 = mybir.dt.float4_e2m1fn_x4
MULT = mybir.AluOpType.mult
COPY = mybir.ActivationFunctionType.Copy
LN = mybir.ActivationFunctionType.Ln

P = 128
PACK = 4
K_PASS = P * PACK
PASSES = TERMS // K_PASS
GROUPS = DIRECTIONS // K_PASS
SCALE_RUN = 128
RUNS = K_PASS // SCALE_RUN
HALF = DOCS // 2
N_TILE = 512
BANKS = 8

ROW_TILES = DIRECTIONS // P
VECTOR_WEIGHS = (3, 5)
EARLY = 6


def tile_latent_term_projection_d4_kernel(
    tc, counts, term_weight, basis_bytes, basis_scale, dir_weight, cat_words, cat_scales, out
):
    nc = tc.nc
    with ExitStack() as ctx:
        keep = ctx.enter_context(tc.tile_pool(name="keep", bufs=1))
        flow = ctx.enter_context(tc.tile_pool(name="flow", bufs=3))
        psum = ctx.enter_context(tc.psum_pool(name="psum", bufs=1))

        ident = keep.tile([P, P], F32, name="ident")
        scale = keep.tile([P, GROUPS, PACK, TERMS // SCALE_RUN], F32, name="scale")
        weight_rows = keep.tile([P, K_PASS], BF16, name="weight_rows")
        weights = keep.tile([P, PASSES + GROUPS, PACK], BF16, name="weights")
        dir_factor = keep.tile([P, GROUPS, PACK], F32, name="dir_factor")
        a_codes = keep.tile([P, PASSES, DOCS], U32, name="a_codes", align_bytes=64)
        a_scales = keep.tile([P, PASSES, DOCS], U8, name="a_scales", align_bytes=64)
        d_codes = keep.tile([P, GROUPS, DOCS], U32, name="d_codes", align_bytes=64)
        d_scales = keep.tile([P, GROUPS, DOCS], U8, name="d_scales", align_bytes=64)
        d_planes = [keep.tile([P, PACK, DOCS], BF16, name="d_planes%d" % gr) for gr in range(GROUPS)]
        d_words = [keep.tile([P, DOCS, PACK], BF16, name="d_words%d" % gr, align_bytes=64) for gr in range(GROUPS)]
        cat = keep.tile([P, GROUPS, 2 * CATEGORIES], U8, name="cat", align_bytes=64)
        cat_planes = keep.tile([P, GROUPS, CATEGORIES], U8, name="cat_planes", align_bytes=64)

        units = [((rt, g), (rt + 1, g)) for g in range(PASSES) for rt in range(0, EARLY, 2)]
        n_early = len(units)
        units += [((rt, g), (rt, g + 1)) for rt in range(EARLY, ROW_TILES) for g in range(0, PASSES, 2)]
        place = {tile_of: (n, h) for n, unit in enumerate(units) for h, tile_of in enumerate(unit)}
        b_codes = keep.tile([P, len(units), 2 * P], U32, name="b_codes", align_bytes=64)
        b_scales = keep.tile([P, len(units), 2 * P], U8, name="b_scales", align_bytes=64)

        free_banks = ["bank%d" % i for i in range(BANKS)]
        bank_of = {}

        def take_bank(key, shape):
            bank_of[key] = free_banks.pop(0)
            return psum.tile(shape, F32, name="psum_tile", tag=bank_of[key])

        def give_bank(key):
            free_banks.append(bank_of[key])

        byte_run, raw = {}, {}
        bytes_view = basis_bytes.rearrange("(gr m j) k -> gr m j k", gr=GROUPS, j=PACK)
        counts_view = counts.rearrange("(g p t) w -> g p t w", p=P, t=PACK)

        def load_bytes(gr, j0, j1, k0, k1):
            held = keep.tile([P, j1 - j0, k1 - k0], U8, name="bytes_%d_%d_%d" % (gr, j0, k0))
            nc.sync.dma_start(out=held[:], in_=bytes_view[gr, :, j0:j1, k0:k1])
            for j in range(j0, j1):
                for k in range(k0, k1, SCALE_RUN):
                    byte_run[(PACK * gr + j, k // SCALE_RUN)] = held[:, j - j0, k - k0 : k - k0 + SCALE_RUN]

        def load_counts(g, parts=1):
            raw[g] = flow.tile([P, PACK, DOCS], BF16, name="raw", tag="stream", bufs=PASSES)
            for i in range(parts):
                rows = slice(i * PACK // parts, (i + 1) * PACK // parts)
                nc.sync.dma_start(out=raw[g][:, rows, :], in_=counts_view[g, :, rows, :])

        logs, a_words = {}, {}

        def take_log(g, i):
            if i == 0:
                logs[g] = flow.tile([P, PACK, DOCS], F32, name="logs", tag="logs", bufs=3)
            rows = slice(2 * i, 2 * i + 2)
            nc.scalar.activation(out=logs[g][:, rows, :], in_=raw[g][:, rows, :], func=LN, bias=1.0, scale=1.0)

        def weigh_terms(g, i):
            if i == 0:
                a_words[g] = flow.tile([P, DOCS, PACK], BF16, name="a_words", tag="a_words", bufs=3, align_bytes=64)
            docs = slice(i * HALF, (i + 1) * HALF)
            nc.vector.tensor_tensor(
                out=a_words[g][:, docs, :].rearrange("p (c i) t -> p c t i", i=4),
                in0=logs[g][:, :, docs].rearrange("p t (c i) -> p c t i", i=4),
                in1=weights[:, g, :].unsqueeze(1).unsqueeze(3).to_broadcast([P, HALF // 4, PACK, 4]),
                op=MULT,
            )

        def quantize_a(g):
            nc.vector.quantize_mx(
                out=a_codes[:, g, :].bitcast(E4M3),
                scales=a_scales[:, g, :],
                in_=a_words[g][:].rearrange("p w t -> p (w t)"),
            )

        wide, turned, grouped = {}, {}, {}

        def on_scalar(n, h):
            if n < n_early:
                return h == 1 and n % 3 != 0
            return h == 1 and n % 2 == 1 and n < len(units) - 2

        def widen(n):
            wide[n] = flow.tile([P, 2, K_PASS], BF16, name="wide", tag="wide", bufs=4)
            for h, (rt, g) in enumerate(units[n]):
                gr, j = divmod(rt, PACK)
                by_parity = wide[n][:, h, :].rearrange("p (u w e) -> p w u e", u=2, e=2)
                for q in range(RUNS):
                    run = RUNS * g + q
                    values = byte_run[(rt, run)].bitcast(FP8)
                    factor = scale[:, gr, j, run : run + 1]
                    if on_scalar(n, h):
                        terms = slice(q * SCALE_RUN, (q + 1) * SCALE_RUN)
                        nc.scalar.activation(out=wide[n][:, h, terms], in_=values, func=COPY, scale=factor)
                    else:
                        word_pairs = slice(q * SCALE_RUN // 4, (q + 1) * SCALE_RUN // 4)
                        nc.vector.tensor_scalar(
                            out=by_parity[:, word_pairs, :, :],
                            in0=values.rearrange("p (w u e) -> p w u e", u=2, e=2),
                            scalar1=factor,
                            scalar2=None,
                            op0=MULT,
                        )

        def turn(n):
            turned[n] = take_bank(("turned", n), [P, 2, 2, P])
            for h in range(2):
                words = wide[n][:, h, :].bitcast(F32)
                for u in range(2):
                    picked = words[:, u : 2 * P : 2] if on_scalar(n, h) else words[:, u * P : (u + 1) * P]
                    nc.tensor.transpose(turned[n][:, h, u, :], picked, ident[:])

        def collect(n):
            grouped[n] = flow.tile([P, 2, P, PACK], BF16, name="grouped", tag="grouped", bufs=6, align_bytes=64)
            words = grouped[n][:].rearrange("p h r t -> p (h r t)").bitcast(F32)
            nc.scalar.copy(
                out=words.rearrange("p (h r u) -> p h r u", h=2, u=2), in_=turned[n][:].rearrange("p h u r -> p h r u")
            )
            give_bank(("turned", n))

        def quantize_b(n):
            nc.vector.quantize_mx(
                out=b_codes[:, n, :].bitcast(E4M3),
                scales=b_scales[:, n, :],
                in_=grouped[n][:].rearrange("p h r t -> p (h r t)"),
            )

        z = {}

        def multiply(rt, g, docs):
            n, h = place[(rt, g)]
            cols = slice(h * P, (h + 1) * P)
            key = (rt, docs.start)
            if g == 0:
                z[key] = take_bank(key, [P, docs.stop - docs.start])
            nc.tensor.matmul_mx(
                out=z[key][:],
                lhsT=b_codes[:, n, cols].bitcast(E4M3),
                lhsT_scale=b_scales[:, n, cols],
                rhs=a_codes[:, g, docs].bitcast(E4M3),
                rhs_scale=a_scales[:, g, docs],
                start=(g == 0),
                stop=(g == PASSES - 1),
            )

        all_docs, first_docs, second_docs = slice(0, DOCS), slice(0, HALF), slice(HALF, DOCS)

        def multiply_unit(n):
            for rt, g in units[n]:
                multiply(rt, g, all_docs if rt < EARLY else first_docs)

        def weigh_directions(rt, docs):
            gr, j = divmod(rt, PACK)
            key = (rt, docs.start)
            plane = d_planes[gr][:, j, docs]
            factor = dir_factor[:, gr, j : j + 1]
            if rt in VECTOR_WEIGHS:
                nc.vector.tensor_scalar(out=plane, in0=z[key][:], scalar1=factor, scalar2=None, op0=MULT)
            else:
                nc.scalar.activation(out=plane, in_=z[key][:], func=COPY, scale=factor)
            give_bank(key)

        def interleave_d(gr, docs):
            nc.vector.tensor_copy(
                out=d_words[gr][:, docs, :].rearrange("p (c i) j -> p c j i", i=4),
                in_=d_planes[gr][:, :, docs].rearrange("p j (c i) -> p c j i", i=4),
            )

        def quantize_d(gr, docs):
            nc.vector.quantize_mx(
                out=d_codes[:, gr, docs].bitcast(E4M3),
                scales=d_scales[:, gr, docs],
                in_=d_words[gr][:, docs, :].rearrange("p w j -> p (w j)"),
            )

        results = {}

        def score(i):
            row_tile, col_tile = divmod(i, CATEGORIES // N_TILE)
            rows = slice(row_tile * P, (row_tile + 1) * P)
            cols = slice(col_tile * N_TILE, (col_tile + 1) * N_TILE)
            acc = take_bank(("score", i), [P, N_TILE])
            for gr in range(GROUPS):
                nc.tensor.matmul_mx(
                    out=acc[:],
                    lhsT=d_codes[:, gr, rows].bitcast(E4M3),
                    lhsT_scale=d_scales[:, gr, rows],
                    rhs=cat[:, gr, 2 * cols.start : 2 * cols.stop].bitcast(E2M1),
                    rhs_scale=cat_planes[:, gr, cols],
                    start=(gr == 0),
                    stop=(gr == GROUPS - 1),
                )
            if i % 2 == 0:
                results[i // 2] = flow.tile([P, 2, N_TILE], F32, name="results", tag="stream", bufs=PASSES)
            result = results[i // 2][:, i % 2, :]
            if i % 2 == 0:
                nc.scalar.copy(out=result, in_=acc[:])
            else:
                nc.vector.tensor_copy(out=result, in_=acc[:])
            give_bank(("score", i))
            nc.sync.dma_start(out=out[rows, cols], in_=result)

        with tc.manual_schedule():
            nc.vector.memset(weight_rows[:], 0.0)
            load_bytes(0, 0, 2, 0, K_PASS)
            nc.scalar.dma_start(out=weight_rows[0:PASSES, :], in_=term_weight.rearrange("(g n) -> g n", g=PASSES))
            nc.scalar.dma_start(
                out=weight_rows[PASSES : PASSES + GROUPS, :], in_=dir_weight.rearrange("(g n) -> g n", g=GROUPS)
            )
            nc.scalar.dma_start(out=scale[:], in_=basis_scale.rearrange("(g m j) b -> m g j b", g=GROUPS, j=PACK))
            load_counts(0, parts=2)
            load_bytes(0, 2, 4, 0, K_PASS)
            load_bytes(1, 0, 2, 0, K_PASS)
            load_counts(1)
            load_bytes(0, 0, 4, K_PASS, 2 * K_PASS)
            load_bytes(1, 0, 2, K_PASS, 2 * K_PASS)
            load_counts(2)
            for g in range(2, PASSES, 2):
                load_bytes(0, 0, 4, g * K_PASS, (g + 2) * K_PASS)
                load_bytes(1, 0, 2, g * K_PASS, (g + 2) * K_PASS)
                for later in range(g + 1, min(g + 3, PASSES)):
                    load_counts(later)
            for k0 in (0, TERMS // 2):
                load_bytes(1, 2, 4, k0, k0 + TERMS // 2)
            nc.sync.dma_start(
                out=cat[:].rearrange("p g n -> p (g n)").bitcast(I32).rearrange("p (g n) -> p g n", g=GROUPS),
                in_=cat_words.bitcast(I32).rearrange("g p n -> p g n"),
            )
            scale_words = cat_planes[:].rearrange("p g n -> p (g n)").bitcast(I32)
            nc.vector.memset(scale_words, 0)
            for quadrant in range(4):
                nc.sync.dma_start(
                    out=scale_words[32 * quadrant : 32 * quadrant + 4, :].rearrange("p (g n) -> p g n", g=GROUPS),
                    in_=cat_scales[:, 4 * quadrant : 4 * quadrant + 4, :].bitcast(I32).rearrange("g q n -> q g n"),
                )
            make_identity(nc, ident[:])

            row_words = weight_rows[:].bitcast(F32)
            turned_rows = take_bank("turned_rows", [P, 2, P])
            for u in range(2):
                nc.tensor.transpose(turned_rows[:, u, :], row_words[:, u : 2 * P : 2], ident[:])

            widen(0)
            take_log(0, 0)
            take_log(0, 1)
            widen(1)
            nc.vector.tensor_copy(
                out=weights[:].rearrange("p g t -> p (g t)").bitcast(F32).rearrange("p (g u) -> p g u", u=2),
                in_=turned_rows[:, :, 0 : PASSES + GROUPS].rearrange("p u g -> p g u"),
            )
            give_bank("turned_rows")
            for s in range(n_early):
                g, third = divmod(s, 3)
                turn(s)
                if third == 1:
                    weigh_terms(g, 0)
                if third == 0 and g > 0:
                    quantize_a(g - 1)
                if third == 0 and g + 1 < PASSES:
                    take_log(g + 1, 0)
                if s >= 1:
                    collect(s - 1)
                if s >= 3:
                    quantize_b(s - 3)
                if third == 1:
                    weigh_terms(g, 1)
                if third == 1 and g + 1 < PASSES:
                    take_log(g + 1, 1)
                widen(s + 2)
                if s >= 4:
                    multiply_unit(s - 4)
            quantize_a(PASSES - 1)
            nc.vector.tensor_copy(out=dir_factor[:], in_=weights[:, PASSES:, :])

            last = len(units) - 1
            pause = last - 2
            for s in range(n_early, len(units)):
                turn(s)
                if s + 2 <= last:
                    widen(s + 2)
                collect(s - 1)
                if s in (n_early + 4, n_early + 5):
                    weigh_directions(s - n_early - 4, all_docs)
                quantize_b(s - 3)
                if n_early < s < pause:
                    multiply_unit(s - 5)
                elif s > pause:
                    multiply_unit(s - 6)
            weigh_directions(2, all_docs)
            collect(last)
            quantize_b(last - 2)
            weigh_directions(3, all_docs)
            quantize_b(last - 1)
            for n in range(last - 5, last - 1):
                multiply_unit(n)
            weigh_directions(6, first_docs)
            weigh_directions(4, all_docs)
            quantize_b(last)
            weigh_directions(5, all_docs)
            multiply_unit(last - 1)
            multiply_unit(last)
            weigh_directions(7, first_docs)

            quarter = [slice(i * P, (i + 1) * P) for i in range(DOCS // P)]
            interleave_d(0, quarter[0])
            interleave_d(0, quarter[1])
            quantize_d(0, quarter[0])
            interleave_d(1, quarter[0])
            quantize_d(0, quarter[1])
            quantize_d(1, quarter[0])
            interleave_d(1, quarter[1])
            interleave_d(0, quarter[2])
            quantize_d(1, quarter[1])
            interleave_d(0, quarter[3])

            for g in range(PASSES):
                multiply(6, g, second_docs)
            for g in range(PASSES // 2):
                multiply(7, g, second_docs)
            weigh_directions(6, second_docs)
            for i in range(4):
                score(i)
            for g in range(PASSES // 2, PASSES):
                multiply(7, g, second_docs)
            for i in range(4, 6):
                score(i)
            weigh_directions(7, second_docs)
            quantize_d(0, quarter[2])
            quantize_d(0, quarter[3])
            interleave_d(1, quarter[2])
            quantize_d(1, quarter[2])
            for i in range(6, 8):
                score(i)
            interleave_d(1, quarter[3])
            quantize_d(1, quarter[3])
            for i in range(8, (DOCS // P) * (CATEGORIES // N_TILE)):
                score(i)
